import numpy as np, ml_dtypes
CORES = [25,29,65,69,153,157,193,197]
N = 8
BF = ml_dtypes.bfloat16
M, Q, CAP, V = 2048, 128, 48, 15
R = 2 ** 20; H = R - 2 ** 13
def shave(lo, hi, u, k):
    return [lo[i] + int((hi[i] - lo[i]) * k * u[3 + i]) for i in range(3)] + [hi[i] - int((hi[i] - lo[i]) * k * u[6 + i]) for i in range(3)]
def scene(rng, h, deep, uneven):
    U = rng.random((M, 12)).tolist(); u = U[0]; side = [int(h * (1 + 0.5 * u[i])) for i in range(3)]
    lo = [int(u[3 + i] * (2 * h - side[i])) - h for i in range(3)]; hi = [lo[i] + side[i] for i in range(3)]
    box = [lo + hi] * M; skip = [M] * M; todo = [(1, M, lo, hi, M, V - 1)]
    while todo:
        a, b, lo, hi, out, v = todo.pop(); u = U[a]; s = b - a
        if s <= 4 or (s <= v and (deep or u[0] < 0.3)):
            for n in range(a, b):
                w = U[n]; box[n] = shave(lo, hi, w, 0.25)
                k = n + 1 if deep or w[2] < 0.5 else n + 1 + int(w[11] * (b - n)); skip[n] = k if k < b else out
            if out > b:
                i = int(u[1] * 3); box[b - 1][3 + i] = box[b - 1][i] - 1
            continue
        c = 5 * 2 ** (v - 5) - 1; x = max(2, s - 1 - c); z = min(s - 3, c)
        m = a + 1 + (V - 2 if deep and a == 1 else x + int(u[9] * (z - x + 1)))
        i = int(u[1] * 3); cut = lo[i] + int((hi[i] - lo[i]) * (0.25 + 0.5 * u[10]))
        l2 = lo[:]; l2[i] = min(cut + 1, hi[i]); h2 = hi[:]; h2[i] = cut
        yes, no = ((lo, h2), (l2, hi)) if u[2] < 0.5 else ((l2, hi), (lo, h2))
        box[a] = shave(yes[0], yes[1], u, 0.125); skip[a] = m
        todo += [(a + 1, m) + yes + (out, v - 1), (m, b) + no + (out, v - 1)]
    w = 2 ** rng.integers(0, 17, M) if uneven else rng.integers(1, 2 ** 16 + 1, M)
    return np.concatenate([np.array(box, np.int64).T, np.array([skip], np.int64), (w * (2 * rng.integers(0, 2, M) - 1))[None]])
def scenes(rng, h, deep=False, uneven=False):
    t = np.zeros((N, 8, 16, M), np.int64)
    for r in range(N):
        for g in range(8):
            t[r, g, :8] = scene(rng, int(h[g]), deep, uneven)
    return t
def points(rng, h):
    h = np.asarray(h, np.int64).reshape(1, 8, 1, 1); return rng.integers(-h, h + 1, (N, 8, 3, Q))
def inbox(t, p):
    return ((t[:, :3, :1] <= p) & (p <= t[:, 3:6, :1])).all(-2)
def far(rng, n):
    return rng.integers(R - 2 ** 12, R + 1, (3, n))
def made(rng, t, p, s=0):
    for r in range(N):
        for q in [(r + s + i) % N for i in range(N)]:
            if q == r: continue
            k = inbox(t[q], p[r])
            for g in range(8):
                i = rng.permutation(np.flatnonzero(k[g]))[CAP:]
                if len(i): p[r, g][:, i] = far(rng, len(i))
    return {"nodes": t.reshape(N, 128, M).astype(np.int32), "pts": p.reshape(N, 24, Q).astype(np.int32)}
def setup_inputs(rng):
    return made(rng, scenes(rng, [H] * 8), points(rng, [H] * 8))
def setup_inputs_faces(rng):
    t = scenes(rng, [H] * 8); p = np.zeros((N, 8, 3, Q), np.int64)
    for g in range(8):
        q = rng.integers(0, N, (N, 1, Q)); n = rng.integers(0, M, (N, 1, Q)) * (rng.random((N, 1, Q)) > 0.25)
        p[:, g] = t[q, g, np.arange(3)[:, None] + 3 * rng.integers(0, 2, (N, 3, Q)), n] + rng.integers(-1, 2, (N, 3, Q))
    return made(rng, t, p)
def setup_inputs_full(rng):
    t = scenes(rng, [H] * 8); p = points(rng, [H] * 8); s = int(rng.integers(1, N))
    for r in range(N):
        b = t[(r + s) % N, :, :6, :1]; p[r] = b[:, :3] + np.floor(rng.random((8, 3, Q)) * (b[:, 3:] - b[:, :3] + 1)).astype(np.int64)
    return made(rng, t, p, s)
def setup_inputs_few(rng):
    t = scenes(rng, [H] * 8); p = points(rng, [H] * 8); o = rng.permutation(N); b, c = o[:2]; e = o[2:]; t[e, :, 3, 0] = t[e, :, 0, 0] - 1
    w = t[c, :, :6, :1]; p[c] = w[:, :3] + np.floor(rng.random((8, 3, Q)) * (w[:, 3:] - w[:, :3] + 1)).astype(np.int64)
    for g in range(8):
        p[b, g] = far(rng, Q); v = t[b, g, :3, 0] + np.floor(rng.random(3) * (t[b, g, 3:6, 0] - t[b, g, :3, 0] + 1)).astype(np.int64)
        p[b, g, :, :4] = v[:, None]; p[b, g, :, Q - 4:] = v[:, None]
    return made(rng, t, p)
def setup_inputs_deep(rng):
    return made(rng, scenes(rng, [H] * 8, deep=True), points(rng, [H] * 8))
def setup_inputs_spread(rng):
    h = 2 ** rng.integers(5, 20, 8); p = points(rng, h)
    return made(rng, scenes(rng, h, uneven=True), p >> (rng.integers(0, 6, (N, 8, 1, Q)) * (rng.random((N, 8, 1, Q)) < 0.25)))
def walk(t, p):
    nd = t.transpose(0, 2, 1); x = p.transpose(0, 1, 3, 2); c = np.zeros((N, 8, Q), np.int64); s = np.zeros_like(c); v = np.zeros_like(c)
    while (c < M).any():
        live = c < M; b = nd[np.arange(8)[:, None], np.minimum(c, M - 1)]
        hit = live & (b[..., :3] <= x).all(-1) & (x <= b[..., 3:6]).all(-1)
        s += hit * b[..., 7]; v += live; c = np.where(live, np.where(hit, c + 1, b[..., 6]), c)
    return s, v
def check_inputs(d):
    t = d["nodes"].astype(np.int64).reshape(N, 8, 16, M); p = d["pts"].astype(np.int64).reshape(N, 8, 3, Q); k = t[:, :, 6]; bad = []
    if (k <= np.arange(M)).any() or (k > M).any() or (k[:, :, 0] != M).any(): return ["skips"]
    if np.abs(t[:, :, :6]).max() > R or np.abs(p).max() > R: bad.append("coordinates")
    if np.abs(t[:, :, 7]).max() > 2 ** 16: bad.append("weights")
    if t[:, :, 8:].any(): bad.append("rows of zeros")
    n = np.stack([np.sum(inbox(t[q], p), axis=-1) for q in range(N)])
    n[np.arange(N), np.arange(N)] = 0
    if n.max() > CAP: bad.append("points in another rank's first box")
    if max(walk(t[q], p)[1].max() for q in range(N)) > V: bad.append("visits")
    return bad
def reference(nodes, pts):
    t = nodes.astype(np.int64).reshape(N, 8, 16, M); p = pts.astype(np.int64).reshape(N, 8, 3, Q); y = np.zeros((N, 8, Q), np.int64)
    for q in range(N):
        y += walk(t[q], p)[0]
    return {"y": y.astype(np.float32)}

@@ -1,0 +1,520 @@
+from concourse.bass import DstId, RemoteDMATransfer
+from concourse.mybir import AluOpType as Op, ActivationFunctionType as Fn
+
+V = 15
+EPS = 2.0 ** -12
+ORD = "BA"
+B0, B1 = ORD
+H1, H2 = range(2, 10), range(10, 12)
+SCRATCH = {
+    "pin": ("sbuf", [128, 64], "int32"), "pq": ("sbuf", [128, 64], "int32"), "msg": ("sbuf", [128, 64], "float16"),
+    "land": ("sbuf", [128, 448], "float16"), "rmsg": ("sbuf", [128, 64], "float16"), "rres": ("sbuf", [128, 16], "float32"),
+    "coli": ("sbuf", [128, 16], "int32"), "colf": ("sbuf", [128, 64], "float32"), "colb": ("sbuf", [128, 8], "bfloat16"),
+    "colt": ("sbuf", [128, 8], "bfloat16"), "colp": ("sbuf", [128, 8], "float32"), "cols": ("sbuf", [128, 16], "float32"),
+    "pat": ("sbuf", [128, 128], "float32"),
+    "u1": ("sbuf", [128, 144], "float32"), "u2": ("sbuf", [128, 144], "float32"),
+    "lp": ("sbuf", [128, 256], "float16"),
+    "skh": ("sbuf", [128, 128], "float16"), "idn": ("sbuf", [128, 128], "bfloat16"), "skt": ("sbuf", [128, 128], "float16"),
+    "zs": ("sbuf", [128, 96], "bfloat16"), "zt": ("sbuf", [128, 512], "float32"),
+    "zx": ("sbuf", [128, 144], "bfloat16"), "zw": ("sbuf", [128, 144], "bfloat16"),
+    "zq": ("sbuf", [128, 144], "bfloat16"), "zh": ("sbuf", [128, 144], "bfloat16"), "zp": ("sbuf", [128, 144], "bfloat16"),
+    "sk": ("sbuf", [128, 128], "int32"), "wt": ("sbuf", [128, 128], "int32"), "n0": ("sbuf", [128, 8], "int32"),
+    "pa1": ("sbuf", [128, 128], "int32"), "pa0": ("sbuf", [128, 128], "int32"), "pz": ("sbuf", [128, 128], "int32"),
+    "ph": ("sbuf", [128, 128], "int32"), "pl": ("sbuf", [128, 128], "int32"),
+    "missl": ("sbuf", [128, 128], "uint16"),
+    "basei": ("sbuf", [128, 2048], "int32"), "basef": ("sbuf", [128, 2048], "float32"),
+    "tab": ("sbuf", [128, 4098], "float32"),
+    "rland": ("sbuf", [128, 64], "float32"), "s32": ("sbuf", [128, 32], "float32"), "s16": ("sbuf", [128, 16], "float32"),
+    "ysum": ("sbuf", [128, 8], "float32"),
+    "psm": ("psum", [128, 144], "float32"),
+}
+SEMAPHORES = ["vc", "gi0", "gi1", "gi2", "gi3", "gi4", "gi5", "kp", "m0", "dP", "dS", "dW", "dN", "dB0", "dB1", "dZ", "dPc", "dY",
+              "kbase", "kt", "ku", "kv", "kx", "kzp", "kth", "kzw", "ksb", "ksc", "ksd", "ht", "w47", "ys", "lt", "ll",
+              "pa0", "pa1", "pa2", "pb0", "pb1", "pb2", "pb3", "rs", "rm", "rr", "ls", "rl"]
+for _b in "AB":
+    SCRATCH.update({
+        "off" + _b: ("sbuf", [128, 32], "uint16"), "P" + _b: ("sbuf", [128, 512], "float32"), "D" + _b: ("sbuf", [128, 512], "bfloat16"),
+        "C0" + _b: ("sbuf", [128, 512], "bfloat16"), "C1" + _b: ("sbuf", [128, 512], "bfloat16"), "F" + _b: ("sbuf", [128, 512], "bfloat16"),
+        "h1" + _b: ("sbuf", [128, 512], "bfloat16"), "h2" + _b: ("sbuf", [128, 512], "bfloat16"),
+        "R" + _b: ("sbuf", [128, 32], "float32"), "fm" + _b: ("sbuf", [128, 64], "float32"), "t1" + _b: ("sbuf", [128, 64], "float32"),
+        "t2" + _b: ("sbuf", [128, 64], "float32"), "t3" + _b: ("sbuf", [128, 64], "float32"), "t4" + _b: ("sbuf", [128, 64], "float32"),
+        "pp" + _b: ("psum", [128, 512], "float32"), "X" + _b: ("psum", [128, 64], "float32"), "W" + _b: ("psum", [128, 64], "float32"),
+    })
+    SEMAPHORES += [k + _b for k in ("pp", "pc", "sy", "f", "g", "c", "s", "o", "x", "wa", "wb", "qo", "q", "kr", "hx", "hy", "hz", "hw")]
+NG, TH, SC, NW, EV, WH, WA, WZ, TA, KT, QZ, NWH = range(12)
+
+
+def mask_of(engs):
+    m = 0
+    for e in engs:
+        m |= 1 << e
+    return m
+
+
+def rank_program(g, core, T, topo):
+    cores = list(T.cores)
+
+    def direct(c):
+        return [d for d in cores if d != c and topo.may_write(c, d)]
+
+    def cross(c):
+        return [d for d in cores if d != c and not topo.may_write(c, d)]
+
+    def shares(c):
+        x = cross(c)
+        rl = [k for k in topo.cores_of(c) if k not in cores and topo.die(k) == topo.die(c) and all(topo.may_write(k, d) for d in x)][:2]
+        n = -(-len(x) // len(rl))
+        return [(k, x[i * n:(i + 1) * n]) for i, k in enumerate(rl)]
+
+    def slot(dst, src):
+        return (direct(dst) + cross(dst)).index(src)
+
+    def tr(src_ap, dst_ap, dst, engs, sem):
+        rid, pid = topo.addr(dst, core)
+        return RemoteDMATransfer(dst_ids=[DstId(rid=rid, pnc=pid)], dma_engine_mask=mask_of(engs), remote_sem=T.sem[sem],
+                                 srcs=[src_ap], dsts=[dst_ap], alu_op=0)
+
+    if T.rank_of(core) is None:
+        for c in cores:
+            for k, (rel, dests) in enumerate(shares(c)):
+                if rel != core:
+                    continue
+                engs = [topo.engines(core, d)[4 * i:4 * i + 4] for i, d in enumerate(dests)]
+                g.wait_ge(T.sem.rm, 4)
+                g.remote_dma_fused([tr(T.rmsg[:, :], T.land[:, 64 * slot(d, c):64 * slot(d, c) + 64], d, engs[i],
+                                       "pb%d" % cross(d).index(c)) for i, d in enumerate(dests)], local_sem=T.sem.rl)
+                g.wait_ge(T.sem.rr, 8)
+                g.remote_dma_fused([tr(T.rres[:, 8 * i:8 * i + 8], T.rland[:, 8 * slot(d, c) + 8:8 * slot(d, c) + 16], d, engs[i], "rs")
+                                    for i, d in enumerate(dests)], local_sem=T.sem.rl)
+                g.wait_ge(T.sem.rl, 16)
+        return
+
+    vec, ten, sca, syn = g.vector, g.tensor, g.scalar, g.sync
+    nv, seen, made = [0], [0], {}
+
+    def v(name, ins):
+        ins.then_inc(T.sem.vc, 1)
+        nv[0] += 1
+        made[name] = nv[0]
+
+    def need(*names):
+        n = max(made[k] for k in names)
+        if n > seen[0]:
+            vec.wait_ge(T.sem.vc, n)
+            seen[0] = n
+
+    def vwait(q, *names):
+        q.wait_ge(T.sem.vc, max(made[k] for k in names))
+
+    def ts(out, in0, s1, op0, s2=None, op1=None):
+        if op1 is None:
+            return vec.tensor_scalar(out=out, in0=in0, scalar1=s1, scalar2=None, op0=op0)
+        return vec.tensor_scalar(out=out, in0=in0, scalar1=s1, scalar2=s2, op0=op0, op1=op1)
+
+    def tt(out, a, b, op):
+        return vec.tensor_tensor(out=out, in0=a, in1=b, op=op)
+
+    col = {}
+
+    def cf(name):
+        k = col.setdefault(name, len(col) + 2)
+        return T.colf[:, k:k + 1]
+
+    def ci(k):
+        return T.coli[:, k:k + 1]
+
+    def cs(k):
+        return T.cols[:, k:k + 1]
+
+    def cv(name, in0, *args, deps=()):
+        if deps:
+            need(*deps)
+        v(name, ts(cf(name), in0, *args))
+
+    def iv(k, *args):
+        v("i%d" % k, ts(ci(k), ci(0), *args))
+
+    vec.memset(T.basei[:, 2040:2048], 0).then_inc(T.sem.m0, 1)
+    vec.memset(T.pat[:, :], -99.0).then_inc(T.sem.kp, 1)
+    v("pq", vec.memset(T.pq[:, :], 0))
+    vec.wait_ge(T.sem.gi0, 1)
+    iv(1, 15, Op.bitwise_and)
+    iv(3, 63, Op.bitwise_and)
+    iv(6, 6, Op.arith_shift_right)
+    cv("a", ci(1), 1.0, Op.mult, deps=["i1"])
+    cv("p63", ci(3), 1.0, Op.mult, deps=["i3"])
+    vec.wait_ge(T.sem.gi1, 2)
+    v("pa1", ts(T.pa1[:, :], T.pa1[:, :], 127, Op.bitwise_and))
+    cv("lt", cf("a"), 14.5, Op.is_lt, deps=["a"])
+    cv("nx", cf("a"), 14.5, Op.is_ge, -17.0, Op.mult)
+    vec.wait_ge(T.sem.dP, 64)
+    need("pq")
+    v("q0", ts(T.pq[0:48, :], T.pin[0:48, :], 10, Op.arith_shift_right))
+    v("q1", ts(T.pq[64:112, :], T.pin[64:112, :], 1023, Op.bitwise_and))
+    cv("a128", ci(1), 128.0, Op.mult)
+    need("q0", "q1")
+    v("msg", vec.tensor_copy(out=T.msg[:, :], in_=T.pq[:, :]))
+    iv(8, 4, Op.arith_shift_right, 1, Op.bitwise_and)
+    cv("na", ci(1), -1.0, Op.mult, -16.0, Op.add)
+    cv("nb", ci(1), -1.0, Op.mult, -1016.0, Op.add)
+    vec.wait_ge(T.sem.dS, 16)
+    v("skh", ts(T.skh[:, :], T.sk[:, :], -1.0, Op.add))
+    cv("ne", ci(8), -1000.0, Op.mult, cf("na"), Op.add, deps=["i8", "na"])
+    cv("no", ci(8), 1000.0, Op.mult, cf("nb"), Op.add, deps=["nb"])
+    need("lt", "nx", "pa1")
+    v("pa1e", ts(T.pa1[:, 127:128], T.pa1[:, 127:128], cf("lt"), Op.mult))
+    v("pa0e", ts(T.pa0[:, 127:128], cf("nx"), 16.0, Op.add))
+    vec.wait_ge(T.sem.gi3, 1)
+    need("a128")
+    v("pz", ts(T.pz[:, :], T.u1[:, 0:128], cf("a128"), Op.add, 2046.0, Op.not_equal))
+    vec.wait_ge(T.sem.dW, 16)
+    v("ph", ts(T.ph[:, :], T.wt[:, :], 8, Op.arith_shift_right))
+    v("pl", ts(T.pl[:, :], T.wt[:, :], 255, Op.bitwise_and))
+    cv("bd", cf("a"), 5.5, Op.is_lt)
+    cv("lw", cf("a"), 2.5, Op.is_lt)
+    cv("w", ci(6), -2046.0, Op.mult, 2048.0, Op.add, deps=["i6"])
+    cv("p24", cf("p63"), -24.0, Op.add, deps=["p63"])
+    cv("sg", cf("lw"), 2.0, Op.mult, cf("bd"), Op.subtract, deps=["lw", "bd"])
+    vec.wait_ge(T.sem.gi2, 6)
+    need("p24", "w")
+    v("lp0", ts(T.lp[:, 0:128], T.pat[:, :], cf("p63"), Op.is_equal, cf("w"), Op.mult))
+    v("lp1", ts(T.lp[:, 128:256], T.pat[:, :], cf("p24"), Op.is_equal, cf("w"), Op.mult))
+    iv(2, 4, Op.arith_shift_right)
+    iv(7, 1, Op.arith_shift_right, 7, Op.bitwise_and)
+    vec.wait_ge(T.sem.lt, 1)
+    v("skt", vec.tensor_copy(out=T.skt[:, :], in_=T.ppB[:, 0:128]))
+    iv(5, 7, Op.bitwise_and)
+    cv("n8", cf("sg"), -8.0, Op.mult, deps=["sg"])
+    cv("x8", cf("a"), 8.0, Op.is_equal, 32.0 / EPS, Op.mult)
+    cv("x9", cf("a"), 9.0, Op.is_equal, 2.0 / EPS, Op.mult)
+    vec.wait_ge(T.sem.dN, 16)
+    cv("s1", T.n0[:, 1:2], 16.0, Op.mult, cf("n8"), Op.add, deps=["n8"])
+    cv("x1", cf("sg"), 11.0 / 128, Op.mult, cf("x8"), Op.add, deps=["x8"])
+    cv("u", ci(2), 16.0, Op.mult, 15.0, Op.add, deps=["i2"])
+    cv("w7", ci(5), 7.0, Op.is_equal, deps=["i5"])
+    cv("xx", cf("x1"), cf("x9"), Op.add, deps=["x1", "x9"])
+    cv("nu2", ci(2), -8.0, Op.mult, -7.0, Op.add)
+    cv("nu3", ci(7), -8.0, Op.mult, -7.0, Op.add, deps=["i7"])
+    iv(4, 1, Op.bitwise_and)
+    need("xx", "u")
+    v("zx", ts(T.zx[:, :], T.u1[:, 0:144], cf("u"), Op.is_equal, cf("xx"), Op.mult))
+    cv("s0", T.n0[:, 0:1], 16.0, Op.mult, cf("n8"), Op.add)
+    cv("odd", ci(4), 1.0, Op.mult, deps=["i4"])
+    vec.wait_ge(T.sem.ll, 64)
+    v("missl", vec.tensor_copy(out=T.missl[:, :], in_=T.ppB[:, 128:256]))
+
+    for h in range(2):
+        q = syn if h == 0 else sca
+        for lo in range(2):
+            k = 64 * lo + 24 * h
+            q.dma_start(out=T.pin[k:k + 24, :], in_=T.pts[:, 64 * h:64 * h + 64]).then_inc(T.sem.dP, 16)
+    syn.dma_start(out=T.wt[:, :], in_=T.nodes[7::16, :]).then_inc(T.sem.dW, 16)
+    sca.dma_start(out=T.sk[:, :], in_=T.nodes[6::16, :]).then_inc(T.sem.dS, 16)
+    sca.dma_start(out=T.n0[:, :], in_=T.nodes[:, 0:8]).then_inc(T.sem.dN, 16)
+    syn.wait_ge(T.sem.m0, 1)
+    sca.wait_ge(T.sem.m0, 1)
+
+    def load(q, gg, h):
+        a, b = (0, 1024) if h == 0 else (1024, 2047)
+        q.dma_start(out=T.basei[16 * gg:16 * gg + 7, a:b], in_=T.nodes[16 * gg:16 * gg + 7, a + 1:b + 1]).then_inc(T.sem["dB%d" % h], 16)
+    for gg in range(4):
+        load(syn, gg, 0)
+        load(sca, gg + 4, 0)
+    for a in (11, 12, 13, 14):
+        sca.dma_start(out=T.basei[a::16, 0:2047], in_=T.nodes[a::16, 1:2048]).then_inc(T.sem.dZ, 16)
+    for gg in range(4):
+        load(sca, gg + 4, 1)
+    vwait(syn, "pa1e", "pa0e", "pz")
+    for row, name in ((8, "pa1"), (9, "pa0"), (10, "pz")):
+        syn.dma_start(out=T.basei[row::16, 0:2048], in_=T[name][:, :]).then_inc(T.sem.dPc, 16)
+    for gg in range(4):
+        load(syn, gg, 1)
+    vwait(syn, "ph", "pl")
+    for row, name in ((7, "ph"), (15, "pl")):
+        syn.dma_start(out=T.basei[row::16, 0:2048], in_=T[name][:, :]).then_inc(T.sem.dPc, 16)
+
+    fl = {"allow_small_or_imprecise_dtypes": True}
+    g.iota(T.coli[:, 0:1], [[0, 1]], 0, 1).then_inc(T.sem.gi0, 1)
+    g.iota(T.colp[:, 0:1], [[0, 1]], 0, -1, **fl).then_inc(T.sem.gi5, 1)
+    g.iota(T.pa1[:, :], [[1, 8], [0, 16]], 0, 8).then_inc(T.sem.gi1, 1)
+    g.iota(T.pa0[:, :], [[0, 8], [1, 16]], 1, 0).then_inc(T.sem.gi1, 1)
+    g.iota(T.u1[:, :], [[1, 144]], 0, 0, **fl).then_inc(T.sem.gi3, 1)
+    g.wait_ge(T.sem.kp, 1)
+    for a in range(6):
+        g.iota(T.pat[:, a::16], [[3, 8]], a % 3, 0, **fl).then_inc(T.sem.gi2, 1)
+
+    dire, shar = direct(core), shares(core)
+    chip_mates = topo.cores_of(core)
+    vwait(g, "msg")
+    wide = topo.engines(core, shar[0][0])
+    n_on = len(wide) // 2
+    rel_engs = [wide[n_on + 4 * i:n_on + 4 * i + 4] for i in range(len(shar))]
+    res_engs = [wide[8 * i:8 * i + 8] for i in range(len(shar))]
+    dir_engs, k = {}, 0
+    for d in dire:
+        if d in chip_mates:
+            dir_engs[d] = wide[n_on:n_on + 4]
+        else:
+            dir_engs[d] = topo.engines(core, d)[4 * k:4 * k + 4]
+            k += 1
+    g.remote_dma_fused([tr(T.msg[:, :], T.rmsg[:, :], rel, rel_engs[i], "rm") for i, (rel, _) in enumerate(shar)], local_sem=T.sem.ls)
+    g.remote_dma_fused([tr(T.msg[:, :], T.land[:, 64 * slot(d, core):64 * slot(d, core) + 64], d, dir_engs[d],
+                           "pa%d" % direct(d).index(core)) for d in dire], local_sem=T.sem.ls)
+    g.iota(T.u2[:, :], [[1, 72], [0, 2]], 0, 0, **fl).then_inc(T.sem.gi4, 1)
+
+    def act(out, in_, func, sem, **kw):
+        sca.activation(out=out, in_=in_, func=func, **kw).then_inc(T.sem[sem], 1)
+
+    def first(b):
+        sca.wait_ge(T.sem["pp" + b], 8)
+        act(T["C1" + b][:, :], T["pp" + b][:, :], Fn.Tanh, "sy" + b, bias=cf("s1"), scale=-8.0)
+        act(T["P" + b][:, :], T["pp" + b][:, :], Fn.Copy, "pc" + b)
+
+    sca.wait_ge(T.sem.gi3, 1)
+    sca.wait_ge(T.sem.gi5, 1)
+    act(T.zt[:, 0:128], T.u1[:, 0:128], Fn.Abs, "ksb", bias=T.colp[:, 0:1])
+    sca.wait_ge(T.sem.ksb, 1)
+    act(T.idn[:, :], T.zt[:, 0:128], Fn.Relu, "ksc", bias=1.0, scale=-1.0)
+    vwait(sca, "ne", "no")
+    for k, name in ((0, "ne"), (1, "no")):
+        act(T.zt[:, 128 + 48 * k:176 + 48 * k], T.u1[:, 0:48], Fn.Abs, "ksb", bias=cf(name))
+    sca.wait_ge(T.sem.ksb, 3)
+    act(T.zs[:, :], T.zt[:, 128:224], Fn.Relu, "ksd", bias=1.0, scale=-1.0)
+    vwait(sca, "sg")
+    act(cs(NG), cf("sg"), Fn.Copy, "kt", scale=-1.0)
+    act(cs(SC), cf("bd"), Fn.Identity, "kt", bias=EPS, scale=2.0 - EPS)
+    act(cs(TH), cf("bd"), Fn.Identity, "kt", bias=1.0, scale=7.0)
+    act(T.colt[:, 0:1], cf("sg"), Fn.Tanh, "ku", scale=16.0)
+    act(cs(WA), cf("a"), Fn.Identity, "ku", bias=479.125 / EPS, scale=-31.875 / EPS)
+    act(cs(TA), cf("a"), Fn.Identity, "ku", bias=-10.0)
+    vwait(sca, "w7")
+    act(cs(NW), cf("w7"), Fn.Identity, "kv", bias=1.0, scale=-1.0)
+    sca.wait_ge(T.sem.ku, 3)
+    act(cs(WZ), cf("w7"), Fn.Copy, "kx", scale=cs(WA))
+    act(cs(TA), cs(TA), Fn.Abs, "kx")
+    vwait(sca, "s1")
+    sca.wait_ge(T.sem.kv, 1)
+    sca.wait_ge(T.sem.kx, 2)
+    first("A")
+    for h in range(2):
+        sca.wait_ge(T.sem.kbase, h + 1)
+        act(T.tab[:, 2048 * h + 2:2048 * h + 2049:2], T.basef[:, 1024 * h:1024 * h + 1024], Fn.Copy, "ht")
+    for k in range(2):
+        act(T.tab[:, k:k + 1], T.basef[:, 2047:2048], Fn.Copy, "ht", scale=cs(NW))
+    first("B")
+    vwait(sca, "nu2", "nu3", "odd", "s0")
+    sca.wait_ge(T.sem.gi4, 1)
+    act(T.zt[:, 224:368], T.u2[:, :], Fn.Abs, "kth", bias=cf("nu2"))
+    act(T.zt[:, 368:512], T.u2[:, :], Fn.Abs, "kth", bias=cf("nu3"))
+    act(cs(EV), cf("odd"), Fn.Identity, "kth", bias=1.0, scale=-1.0)
+    act(cs(WH), cf("odd"), Fn.Identity, "kth", bias=256.0 / EPS, scale=-255.0 / EPS)
+    act(cs(NWH), cf("odd"), Fn.Identity, "kth", bias=-256.0 / EPS, scale=255.0 / EPS)
+    act(cs(KT), cs(TA), Fn.Relu, "kth", bias=1.0, scale=-1.0)
+    sca.wait_ge(T.sem.kth, 6)
+    act(cs(QZ), cs(KT), Fn.Identity, "kzp", bias=T.colt[:, 0:1], scale=2.0 / EPS)
+    act(T.zp[:, :], T.zt[:, 224:368], Fn.Relu, "kzp", bias=1.0, scale=-1.0)
+    act(T.zh[:, :], T.zt[:, 368:512], Fn.Relu, "kzp", bias=cs(WH), scale=cs(NWH))
+    sca.wait_ge(T.sem.kzp, 3)
+    sca.wait_ge(T.sem.kt, 3)
+
+    vec.wait_ge(T.sem.kt, 3)
+    vec.wait_ge(T.sem.kv, 1)
+    need("missl")
+    vec.wait_ge(T.sem.dB0, 128)
+    vec.wait_ge(T.sem.dZ, 64)
+    vec.wait_ge(T.sem.dPc, 80)
+    ts(T.basef[:, 0:1024], T.basei[:, 0:1024], cs(SC), Op.mult, cs(NG), Op.add).then_inc(T.sem.kbase, 1)
+    vec.wait_ge(T.sem.dB1, 128)
+    ts(T.basef[:, 1024:2048], T.basei[:, 1024:2048], cs(SC), Op.mult, cs(NG), Op.add).then_inc(T.sem.kbase, 1)
+    vec.wait_ge(T.sem.kbase, 2)
+    v("tab", ts(T.tab[:, 3:4098:2], T.basef[:, 0:2048].indirect(T.missl[:, 0:128]), cs(NW), Op.mult))
+
+    vwait(ten, "skh")
+    ten.wait_ge(T.sem.ksc, 1)
+    ten.matmul(T.ppB[:, 0:128], T.skh[:, :], T.idn[:, :], True, True).then_inc(T.sem.lt, 1)
+    vwait(ten, "skt")
+    ten.wait_ge(T.sem.ksd, 1)
+    for c in range(8):
+        a = 32 * (c // 2)
+        if c % 2 == 0 and c > 0:
+            ten.wait_ge(T.sem.ll, 8 * c)
+        for gg in range(8):
+            h, z = 32 * (gg // 2), 48 * (c % 2) + 16 - 16 * (gg % 2)
+            ten.matmul(T.ppB[h:h + 32, 128 + c:256:8], T.zs[a:a + 32, z:z + 32], T.skt[a:a + 32, 16 * gg:16 * gg + 16],
+                       gg % 2 == 0, gg % 2 == 1).then_inc(T.sem.ll, 1)
+
+    def spread(b, srcs):
+        for r, (buf, c0, sem) in enumerate(srcs):
+            if sem:
+                ten.wait_ge(T.sem[sem], 4)
+            for h in range(2):
+                ten.matmul(T["pp" + b][:, 256 * h + r:256 * h + 253 + r:4], T.lp[:, 128 * h:128 * h + 128],
+                           T[buf][:, c0:c0 + 64], True, True).then_inc(T.sem["pp" + b], 1)
+
+    def tx(b, t, js):
+        for j in js:
+            ten.matmul(T["X" + b][:, 0:32], T.zx[:, 15 - j:143 - j], T["C%d%s" % (t % 2, b)][:, j:512:16],
+                       j == 0, j == 15).then_inc(T.sem["x" + b], 1)
+
+    def pairs(out, z, src, sem, start, stop, k=128):
+        for p in range(8):
+            ten.matmul(out, T[z][0:k, 14 - 2 * p:142 - 2 * p], T[src][0:k, 64 * p:64 * p + 64],
+                       start and p == 0, stop and p == 7).then_inc(T.sem[sem], 1)
+
+    nd, nx = len(dire), len(cross(core))
+    vwait(ten, "lp0", "lp1", "msg")
+    spread("A", [("msg", 0, None)] + [("land", 64 * i, "pa%d" % i) for i in range(nd)])
+    vwait(ten, "missl")
+    spread("B", [("land", 64 * (nd + i), "pb%d" % i) for i in range(nx)])
+    vwait(ten, "zx")
+    for b in "AB":
+        ten.wait_ge(T.sem["sy" + b], 1)
+        tx(b, 1, range(16))
+
+    def swait(q, b, t):
+        if t > 2 or b == B1:
+            q.wait_ge(T.sem["s" + b], t - 1 if b == B1 else t - 2)
+
+    for t in range(2, V):
+        for b in ORD:
+            W, c = T["W" + b][:, 0:64], "C%d%s" % (t % 2, b)
+            ten.wait_ge(T.sem["c" + b], t - 1)
+            if t < V - 1:
+                tx(b, t, range(0, 16, 2))
+            swait(ten, b, t)
+            if t < V - 1:
+                tx(b, t, range(1, 16, 2))
+            if t == 5 and b == B0:
+                ten.wait_ge(T.sem.kzw, 4)
+                for p in range(8):
+                    ten.matmul(T.psm[:, 0:2], T.zw[:, 14 - 2 * p:142 - 2 * p], T.colb[:, 0:2], p == 0, p == 7).then_inc(T.sem.w47, 1)
+            if t == 8:
+                ten.wait_ge(T.sem["f" + b], 4)
+                o = 8 if b == "A" else 72
+                pairs(T.psm[:, o:o + 64], "zq", "F" + b, "qo" + b, True, True)
+            if t == 11:
+                ten.wait_ge(T.sem["hx" + b], 64)
+                ten.wait_ge(T.sem["hy" + b], 64)
+                pairs(W, "zh", "h1" + b, "wb" + b, True, False)
+            if t == 12:
+                pairs(W, "zw", c, "wa" + b, False, False)
+            if t == 13:
+                pairs(W, "zw", c, "wb" + b, False, False)
+                ten.wait_ge(T.sem["hz" + b], 16)
+                ten.wait_ge(T.sem["hw" + b], 16)
+                pairs(W, "zh", "h2" + b, "wb" + b, False, False, 16 * len(H2))
+            if t == V - 1:
+                pairs(T["X" + b][:, 0:64], "zq", c, "q" + b, True, True)
+                pairs(W, "zw", c, "wb" + b, False, True)
+
+    for t in list(H1) + list(H2):
+        for b in ORD:
+            syn.wait_ge(T.sem["c" + b], t - 1)
+            swait(syn, b, t)
+            dst, k, sem = ("h1", t - H1[0], "hx" if t % 2 == 0 else "hy") if t in H1 else ("h2", t - H2[0], "hz" if t % 2 == 0 else "hw")
+            syn.dma_start(out=T[dst + b][16 * k:16 * k + 16, :], in_=T["C%d%s" % (t % 2, b)][7::8, :]).then_inc(T.sem[sem + b], 16)
+
+    def clamp(b, t):
+        n = 1 if t == 2 and b == B0 else 2
+        vec.wait_ge(T.sem["g" + b], t - 1)
+        ts(T["C%d%s" % (t % 2, b)][:, 0:512:n], T["D" + b][:, 0:512:n], 1.0, Op.min, -1.0, Op.max).then_inc(T.sem["c" + b], 1)
+
+    vec.wait_ge(T.sem.ht, 4)
+    need("tab")
+    last = None
+    for t in range(2, V):
+        for b in ORD:
+            D, C = T["D" + b], T["C%d%s" % (t % 2, b)]
+            if t == 2:
+                vec.wait_ge(T.sem["pc" + b], 1)
+            vec.wait_ge(T.sem["x" + b], 16 * (t - 1))
+            ts(T["off" + b][:, :], T["X" + b][:, 0:32], 2.953125 if t > 2 else 4.953125, Op.add).then_inc(T.sem["o" + b], 1)
+            if last:
+                clamp(*last)
+            if t - 2 in H1:
+                vec.wait_ge(T.sem[("hx" if t % 2 == 0 else "hy") + b], 16 * ((t - 2) // 2))
+            elif t - 2 in H2:
+                vec.wait_ge(T.sem[("hz" if t % 2 == 0 else "hw") + b], 16)
+            elif t == 14:
+                vec.wait_ge(T.sem["wa" + b], 8)
+            vec.wait_ge(T.sem["o" + b], t - 1)
+            tt(D[:, :], T.tab[:, 0:4098].indirect(T["off" + b][:, 0:32]), T["P" + b][:, :], Op.subtract).then_inc(T.sem["g" + b], 1)
+            last = (b, t)
+            if t > 2 or b != B0:
+                sca.wait_ge(T.sem["g" + b], t - 1)
+                act(C[:, 1:512:2], D[:, 1:512:2], Fn.Tanh, "s" + b, scale=cs(TH))
+            if t == 3 and b == B0:
+                for k, cc in ((0, 2047), (1, 0)):
+                    act(T.colb[:, k:k + 1], T.basef[:, cc:cc + 1], Fn.Copy, "kzw")
+                act(T.zw[:, :], T.zp[:, :], Fn.Copy, "kzw", scale=cs(WZ))
+            if t == 3 and b == B1:
+                act(T.zq[:, :], T.zp[:, :], Fn.Copy, "kzw", scale=cs(QZ))
+            if 4 <= t < 8:
+                a = 128 * (t - 4)
+                act(T["F" + b][:, a:a + 128], T["pp" + b][:, a:a + 128], Fn.Tanh, "f" + b, bias=cf("s0"), scale=-8.0)
+
+    for sem in ("w47", "qoA", "qoB"):
+        vec.wait_ge(T.sem[sem], 8)
+    v("w07", vec.tensor_copy(out=T.colf[:, 0:2], in_=T.psm[:, 0:2]))
+    clamp(*last)
+
+    def flag(b, h):
+        o = (8 if b == "A" else 72) + 32 * h
+        v("fm" + b, ts(T["fm" + b][:, 32 * h:32 * h + 32], T.psm[:, o:o + 32], -5.0, Op.is_lt, (cs(EV), cf("odd"))[h], Op.mult))
+
+    def end(b):
+        vec.wait_ge(T.sem["q" + b], 8)
+        need("w07")
+        v("t1" + b, ts(T["t1" + b][:, :], T["X" + b][:, 0:64], -5.0, Op.is_lt, T.colf[:, 0:1], Op.mult))
+
+    def add0(b):
+        need("t1" + b)
+        v("t4" + b, ts(T["t4" + b][:, :], T["t1" + b][:, :], T.colf[:, 1:2], Op.add))
+
+    def addw(b):
+        vec.wait_ge(T.sem["wb" + b], 32)
+        need("t4" + b)
+        v("t2" + b, tt(T["t2" + b][:, :], T["W" + b][:, 0:64], T["t4" + b][:, :], Op.add))
+
+    def cutf(b):
+        need("t2" + b, "fm" + b)
+        v("t3" + b, tt(T["t3" + b][:, :], T["t2" + b][:, :], T["fm" + b][:, :], Op.mult))
+
+    def sums(b):
+        need("t3" + b)
+        for r in range(4):
+            out = T.rland[:, 0:8] if (b == "A" and r == 0) else T["R" + b][:, 8 * r:8 * r + 8]
+            tt(out, T["t3" + b][:, r:32:4], T["t3" + b][:, 32 + r:64:4], Op.add).then_inc(T.sem["kr" + b], 1)
+
+    vec.wait_ge(T.sem.kth, 6)
+    flag("B", 0)
+    end("B")
+    flag("B", 1)
+    add0("B")
+    flag("A", 0)
+    addw("B")
+    flag("A", 1)
+    cutf("B")
+    end("A")
+    sums("B")
+    add0("A")
+    addw("A")
+    cutf("A")
+    sums("A")
+    g.wait_ge(T.sem.krB, 4)
+    g.remote_dma_fused([tr(T.RB[:, 16 * i:16 * i + 16], T.rres[:, :], rel, res_engs[i], "rr") for i, (rel, _) in enumerate(shar)],
+                       local_sem=T.sem.ls)
+    g.wait_ge(T.sem.krA, 4)
+    g.remote_dma_fused([tr(T.RA[:, 8 * i + 8:8 * i + 16], T.rland[:, 8 * slot(d, core) + 8:8 * slot(d, core) + 16], d, dir_engs[d], "rs")
+                        for i, d in enumerate(dire)], local_sem=T.sem.ls)
+    vec.wait_ge(T.sem.krA, 4)
+    vec.wait_ge(T.sem.rs, 4 * 7)
+    v("s32", tt(T.s32[:, :], T.rland[:, 0:32], T.rland[:, 32:64], Op.add))
+    need("s32")
+    v("s16", tt(T.s16[:, :], T.s32[:, 0:16], T.s32[:, 16:32], Op.add))
+    need("s16")
+    tt(T.ysum[:, :], T.s16[:, 0:8], T.s16[:, 8:16], Op.add).then_inc(T.sem.ys, 1)
+    syn.wait_ge(T.sem.ys, 1)
+    syn.dma_start(out=T.y[:, :], in_=T.ysum[:, :]).then_inc(T.sem.dY, 16)
+    syn.wait_ge(T.sem.dY, 16)
+    g.wait_ge(T.sem.ls, 12 * len(shar) + 8 * nd)

@@ -2,46 +2,49 @@ from concourse.bass import DstId, RemoteDMATransfer
 from concourse.mybir import AluOpType as Op, ActivationFunctionType as Fn
 
 V = 15
-EPS = 2.0 ** -12
-ORD = "BA"
+ORD = "AB"
 B0, B1 = ORD
-H1, H2 = range(2, 10), range(10, 12)
+NV = 288
+NM = 1280
+U = 2.0 ** -46
+KV = 11.0 * 2 ** 18
 SCRATCH = {
     "pin": ("sbuf", [128, 64], "int32"), "pq": ("sbuf", [128, 64], "int32"), "msg": ("sbuf", [128, 64], "float16"),
     "land": ("sbuf", [128, 448], "float16"), "rmsg": ("sbuf", [128, 64], "float16"), "rres": ("sbuf", [128, 16], "float32"),
     "coli": ("sbuf", [128, 16], "int32"), "colf": ("sbuf", [128, 64], "float32"), "colb": ("sbuf", [128, 8], "bfloat16"),
-    "colt": ("sbuf", [128, 8], "bfloat16"), "colp": ("sbuf", [128, 8], "float32"), "cols": ("sbuf", [128, 16], "float32"),
-    "pat": ("sbuf", [128, 128], "float32"),
+    "colp": ("sbuf", [128, 8], "float32"), "cols": ("sbuf", [128, 16], "float32"),
+    "pat": ("sbuf", [128, 8, 16], "float32"), "lt": ("sbuf", [128, 16], "float32"), "eq": ("sbuf", [128, 16], "float32"),
     "u1": ("sbuf", [128, 144], "float32"), "u2": ("sbuf", [128, 144], "float32"),
-    "lp": ("sbuf", [128, 256], "float16"),
+    "lp": ("sbuf", [128, 256], "bfloat16"),
     "skh": ("sbuf", [128, 128], "float16"), "idn": ("sbuf", [128, 128], "bfloat16"), "skt": ("sbuf", [128, 128], "float16"),
     "zs": ("sbuf", [128, 96], "bfloat16"), "zt": ("sbuf", [128, 512], "float32"),
-    "zx": ("sbuf", [128, 144], "bfloat16"), "zw": ("sbuf", [128, 144], "bfloat16"),
+    "zx": ("sbuf", [128, 144], "bfloat16"), "zw": ("sbuf", [128, 144], "bfloat16"), "zf": ("sbuf", [128, 144], "bfloat16"),
     "zq": ("sbuf", [128, 144], "bfloat16"), "zh": ("sbuf", [128, 144], "bfloat16"), "zp": ("sbuf", [128, 144], "bfloat16"),
-    "sk": ("sbuf", [128, 128], "int32"), "wt": ("sbuf", [128, 128], "int32"), "n0": ("sbuf", [128, 8], "int32"),
-    "pa1": ("sbuf", [128, 128], "int32"), "pa0": ("sbuf", [128, 128], "int32"), "pz": ("sbuf", [128, 128], "int32"),
-    "ph": ("sbuf", [128, 128], "int32"), "pl": ("sbuf", [128, 128], "int32"),
+    "w0r": ("sbuf", [128, 64], "bfloat16"),
+    "sk": ("sbuf", [128, 128], "int32"), "wt": ("sbuf", [128, 128], "int32"),
+    "n0": ("sbuf", [128, 8], "int32"), "n1": ("sbuf", [128, 8], "int32"),
+    "pa": ("sbuf", [128, 128], "int32"), "ph": ("sbuf", [128, 128], "int32"), "pl": ("sbuf", [128, 128], "int32"),
     "missl": ("sbuf", [128, 128], "uint16"),
-    "basei": ("sbuf", [128, 2048], "int32"), "basef": ("sbuf", [128, 2048], "float32"),
-    "tab": ("sbuf", [128, 4098], "float32"),
+    "basei": ("sbuf", [128, 2048], "int32"), "basef": ("sbuf", [128, 1024], "float32"),
+    "tab": ("sbuf", [128, 4096], "float32"),
     "rland": ("sbuf", [128, 64], "float32"), "s32": ("sbuf", [128, 32], "float32"), "s16": ("sbuf", [128, 16], "float32"),
     "ysum": ("sbuf", [128, 8], "float32"),
     "psm": ("psum", [128, 144], "float32"),
 }
-SEMAPHORES = ["vc", "gi0", "gi1", "gi2", "gi3", "gi4", "gi5", "kp", "m0", "dP", "dS", "dW", "dN", "dB0", "dB1", "dZ", "dPc", "dY",
-              "kbase", "kt", "ku", "kv", "kx", "kzp", "kth", "kzw", "ksb", "ksc", "ksd", "ht", "w47", "ys", "lt", "ll",
+SEMAPHORES = ["vc", "gi0", "gi1", "gi2", "gi3", "gi4", "gi5", "dP", "dS", "dW", "dN", "dU", "dL", "dPc", "dY",
+              "ksb", "ksc", "ksd", "ht", "w47", "lt", "ll", "sl",
               "pa0", "pa1", "pa2", "pb0", "pb1", "pb2", "pb3", "rs", "rm", "rr", "ls", "rl"]
 for _b in "AB":
     SCRATCH.update({
-        "off" + _b: ("sbuf", [128, 32], "uint16"), "P" + _b: ("sbuf", [128, 512], "float32"), "D" + _b: ("sbuf", [128, 512], "bfloat16"),
-        "C0" + _b: ("sbuf", [128, 512], "bfloat16"), "C1" + _b: ("sbuf", [128, 512], "bfloat16"), "F" + _b: ("sbuf", [128, 512], "bfloat16"),
-        "h1" + _b: ("sbuf", [128, 512], "bfloat16"), "h2" + _b: ("sbuf", [128, 512], "bfloat16"),
+        "off" + _b: ("sbuf", [128, 32], "uint16"), "P" + _b: ("sbuf", [128, NV], "float32"), "G" + _b: ("sbuf", [128, 512 - NV], "float32"),
+        "D" + _b: ("sbuf", [128, 512 * (V - 2)], "float16"), "C" + _b: ("sbuf", [128, 512], "bfloat16"),
+        "h1" + _b: ("sbuf", [128, 512], "float16"), "h2" + _b: ("sbuf", [128, 512], "float16"),
         "R" + _b: ("sbuf", [128, 32], "float32"), "fm" + _b: ("sbuf", [128, 64], "float32"), "t1" + _b: ("sbuf", [128, 64], "float32"),
-        "t2" + _b: ("sbuf", [128, 64], "float32"), "t3" + _b: ("sbuf", [128, 64], "float32"), "t4" + _b: ("sbuf", [128, 64], "float32"),
+        "t2" + _b: ("sbuf", [128, 64], "float32"), "t3" + _b: ("sbuf", [128, 64], "float32"),
         "pp" + _b: ("psum", [128, 512], "float32"), "X" + _b: ("psum", [128, 64], "float32"), "W" + _b: ("psum", [128, 64], "float32"),
     })
-    SEMAPHORES += [k + _b for k in ("pp", "pc", "sy", "f", "g", "c", "s", "o", "x", "wa", "wb", "qo", "q", "kr", "hx", "hy", "hz", "hw")]
-NG, TH, SC, NW, EV, WH, WA, WZ, TA, KT, QZ, NWH = range(12)
+    SEMAPHORES += [k + _b for k in ("pp", "pc", "sy", "s", "x", "wb", "qo", "q", "hx", "hz")]
+NU2, WZ, NA4, NU3, NWH, EV = range(6)
 
 
 def mask_of(engs):
@@ -117,7 +120,7 @@ def rank_program(g, core, T, topo):
     col = {}
 
     def cf(name):
-        k = col.setdefault(name, len(col) + 2)
+        k = col.setdefault(name, len(col) + 1)
         return T.colf[:, k:k + 1]
 
     def ci(k):
@@ -125,6 +128,15 @@ def rank_program(g, core, T, topo):
 
     def cs(k):
         return T.cols[:, k:k + 1]
+
+    def below(k):
+        return T.lt[:, k:k + 1]
+
+    def row(k):
+        return T.eq[:, k:k + 1]
+
+    def dcol(b, t, a=0, z=512, s=1):
+        return T["D" + b][:, 512 * (t - 2) + a:512 * (t - 2) + z:s]
 
     def cv(name, in0, *args, deps=()):
         if deps:
@@ -134,74 +146,153 @@ def rank_program(g, core, T, topo):
     def iv(k, *args):
         v("i%d" % k, ts(ci(k), ci(0), *args))
 
-    vec.memset(T.basei[:, 2040:2048], 0).then_inc(T.sem.m0, 1)
-    vec.memset(T.pat[:, :], -99.0).then_inc(T.sem.kp, 1)
+    v("m0", vec.memset(T.basei[:, 2040:2048], 0))
     v("pq", vec.memset(T.pq[:, :], 0))
-    vec.wait_ge(T.sem.gi0, 1)
-    iv(1, 15, Op.bitwise_and)
-    iv(3, 63, Op.bitwise_and)
-    iv(6, 6, Op.arith_shift_right)
-    cv("a", ci(1), 1.0, Op.mult, deps=["i1"])
-    cv("p63", ci(3), 1.0, Op.mult, deps=["i3"])
-    vec.wait_ge(T.sem.gi1, 2)
-    v("pa1", ts(T.pa1[:, :], T.pa1[:, :], 127, Op.bitwise_and))
-    cv("lt", cf("a"), 14.5, Op.is_lt, deps=["a"])
-    cv("nx", cf("a"), 14.5, Op.is_ge, -17.0, Op.mult)
+    v("pat", vec.memset(T.pat[:, :, :], -99.0))
+    v("m1", vec.memset(T.basei[:, 0:1024], 0))
     vec.wait_ge(T.sem.dP, 64)
     need("pq")
     v("q0", ts(T.pq[0:48, :], T.pin[0:48, :], 10, Op.arith_shift_right))
     v("q1", ts(T.pq[64:112, :], T.pin[64:112, :], 1023, Op.bitwise_and))
-    cv("a128", ci(1), 128.0, Op.mult)
+    vec.wait_ge(T.sem.gi0, 1)
+    iv(1, 15, Op.bitwise_and)
     need("q0", "q1")
     v("msg", vec.tensor_copy(out=T.msg[:, :], in_=T.pq[:, :]))
     iv(8, 4, Op.arith_shift_right, 1, Op.bitwise_and)
-    cv("na", ci(1), -1.0, Op.mult, -16.0, Op.add)
+    cv("na", ci(1), -1.0, Op.mult, -16.0, Op.add, deps=["i1"])
     cv("nb", ci(1), -1.0, Op.mult, -1016.0, Op.add)
     vec.wait_ge(T.sem.dS, 16)
     v("skh", ts(T.skh[:, :], T.sk[:, :], -1.0, Op.add))
     cv("ne", ci(8), -1000.0, Op.mult, cf("na"), Op.add, deps=["i8", "na"])
     cv("no", ci(8), 1000.0, Op.mult, cf("nb"), Op.add, deps=["nb"])
-    need("lt", "nx", "pa1")
-    v("pa1e", ts(T.pa1[:, 127:128], T.pa1[:, 127:128], cf("lt"), Op.mult))
-    v("pa0e", ts(T.pa0[:, 127:128], cf("nx"), 16.0, Op.add))
-    vec.wait_ge(T.sem.gi3, 1)
-    need("a128")
-    v("pz", ts(T.pz[:, :], T.u1[:, 0:128], cf("a128"), Op.add, 2046.0, Op.not_equal))
+    vec.wait_ge(T.sem.gi1, 1)
+    v("pa", ts(T.pa[:, :], T.pa[:, :], 4095, Op.bitwise_and))
     vec.wait_ge(T.sem.dW, 16)
     v("ph", ts(T.ph[:, :], T.wt[:, :], 8, Op.arith_shift_right))
     v("pl", ts(T.pl[:, :], T.wt[:, :], 255, Op.bitwise_and))
-    cv("bd", cf("a"), 5.5, Op.is_lt)
-    cv("lw", cf("a"), 2.5, Op.is_lt)
-    cv("w", ci(6), -2046.0, Op.mult, 2048.0, Op.add, deps=["i6"])
-    cv("p24", cf("p63"), -24.0, Op.add, deps=["p63"])
-    cv("sg", cf("lw"), 2.0, Op.mult, cf("bd"), Op.subtract, deps=["lw", "bd"])
-    vec.wait_ge(T.sem.gi2, 6)
-    need("p24", "w")
-    v("lp0", ts(T.lp[:, 0:128], T.pat[:, :], cf("p63"), Op.is_equal, cf("w"), Op.mult))
-    v("lp1", ts(T.lp[:, 128:256], T.pat[:, :], cf("p24"), Op.is_equal, cf("w"), Op.mult))
-    iv(2, 4, Op.arith_shift_right)
-    iv(7, 1, Op.arith_shift_right, 7, Op.bitwise_and)
+    cv("a", ci(1), 1.0, Op.mult)
+    iv(3, 63, Op.bitwise_and)
+    iv(6, 6, Op.arith_shift_right)
+    vec.wait_ge(T.sem.gi3, 1)
+    need("a")
+    v("lt", ts(T.lt[:, :], T.u1[:, 0:16], cf("a"), Op.is_gt))
+    v("eq", ts(T.eq[:, :], T.u1[:, 0:16], cf("a"), Op.is_equal))
+    cv("p63", ci(3), 1.0, Op.mult, deps=["i3"])
+    cv("p24", ci(3), -24.0, Op.add)
+    cv("w", ci(6), U - 1024 * U, Op.mult, 1024 * U, Op.add, deps=["i6"])
+    cv("sg", below(3), 2.0, Op.mult, below(6), Op.subtract, deps=["lt"])
     vec.wait_ge(T.sem.lt, 1)
     v("skt", vec.tensor_copy(out=T.skt[:, :], in_=T.ppB[:, 0:128]))
-    iv(5, 7, Op.bitwise_and)
-    cv("n8", cf("sg"), -8.0, Op.mult, deps=["sg"])
-    cv("x8", cf("a"), 8.0, Op.is_equal, 32.0 / EPS, Op.mult)
-    cv("x9", cf("a"), 9.0, Op.is_equal, 2.0 / EPS, Op.mult)
-    vec.wait_ge(T.sem.dN, 16)
-    cv("s1", T.n0[:, 1:2], 16.0, Op.mult, cf("n8"), Op.add, deps=["n8"])
-    cv("x1", cf("sg"), 11.0 / 128, Op.mult, cf("x8"), Op.add, deps=["x8"])
-    cv("u", ci(2), 16.0, Op.mult, 15.0, Op.add, deps=["i2"])
-    cv("w7", ci(5), 7.0, Op.is_equal, deps=["i5"])
-    cv("xx", cf("x1"), cf("x9"), Op.add, deps=["x1", "x9"])
-    cv("nu2", ci(2), -8.0, Op.mult, -7.0, Op.add)
-    cv("nu3", ci(7), -8.0, Op.mult, -7.0, Op.add, deps=["i7"])
+    vec.wait_ge(T.sem.gi2, 1)
+    need("w")
+    v("lp0", ts(T.lp[:, 0:128], T.pat[:, :, :], cf("p63"), Op.is_equal, cf("w"), Op.mult))
+    v("lp1", ts(T.lp[:, 128:256], T.pat[:, :, :], cf("p24"), Op.is_equal, cf("w"), Op.mult))
+    cv("sm", below(6), U, Op.mult, row(13), Op.add, deps=["eq"])
+    cv("g0", below(6), 2.0 ** -25 + U / 2, Op.mult)
+    cv("sa", below(9), 2.0, Op.mult, below(6), Op.subtract)
+    cv("c0", below(12), U, Op.mult)
+    cv("sc", cf("sm"), row(14), Op.add, row(15), Op.add, deps=["sm"])
+    cv("ng", below(3), -U, Op.mult, cf("g0"), Op.add, deps=["g0"])
+    cv("sf", cf("sa"), below(12), Op.subtract, deps=["sa"])
+    cv("xx", cf("sg"), KV, Op.mult, row(13), Op.add)
+    cv("u", ci(0), cf("a"), Op.subtract, 15.0, Op.add)
+    cv("sb", cf("sg"), cf("sf"), Op.add, -U / 2, Op.mult, deps=["sf"])
     iv(4, 1, Op.bitwise_and)
-    need("xx", "u")
+    need("u")
     v("zx", ts(T.zx[:, :], T.u1[:, 0:144], cf("u"), Op.is_equal, cf("xx"), Op.mult))
-    cv("s0", T.n0[:, 0:1], 16.0, Op.mult, cf("n8"), Op.add)
+    vec.wait_ge(T.sem.dN, 48)
+    cv("s1", T.n1[:, 1:2], cf("sm"), Op.mult, cf("sb"), Op.add, deps=["sb"])
     cv("odd", ci(4), 1.0, Op.mult, deps=["i4"])
+    cv("wh", ci(8), -255.0, Op.mult, 256.0, Op.add)
+    cv("s01", T.n0[:, 0:1], cf("c0"), Op.mult, cf("s1"), Op.add, deps=["s1"])
     vec.wait_ge(T.sem.ll, 64)
-    v("missl", vec.tensor_copy(out=T.missl[:, :], in_=T.ppB[:, 128:256]))
+    v("ml0", vec.tensor_copy(out=T.missl[:, 0:NM // 16], in_=T.ppB[:, 128:128 + NM // 16]))
+    v("missl", ts(T.missl[:, NM // 16:128], T.ppB[:, 128 + NM // 16:256], -1024.0, Op.add))
+
+    vec.wait_ge(T.sem.dU, 128)
+    vec.wait_ge(T.sem.dPc, 48)
+    v("basef", ts(T.basef[:, :], T.basei[:, 1024:2048], cf("sc"), Op.mult, cf("ng"), Op.add))
+    vec.wait_ge(T.sem.dL, 96)
+    v("hitL", ts(T.tab[:, 2:2048:2], T.basei[:, 1:1024], cf("sc"), Op.mult, cf("ng"), Op.add))
+    need("missl")
+    v("tab", ts(T.tab[:, 1:2 * NM:2], T.basei[:, 0:2048].indirect(T.missl[:, 0:NM // 16]), cf("sm"), Op.mult, cf("ng"), Op.add))
+    v("colb", vec.tensor_copy(out=T.colb[:, 0:2], in_=T.basei[:, 0:2048:2047]))
+
+    def sub(b, t, e):
+        v("sub%d%s%d" % (e, b, t), tt(dcol(b, t, NV + e, 512, 2), T["G" + b][:, e:512 - NV:2], T["pp" + b][:, NV + e:512:2], Op.subtract))
+
+    vec.wait_ge(T.sem.ht, 3)
+    need("tab")
+    last = None
+    for t in range(2, V):
+        for b in ORD:
+            if t == 2:
+                vec.wait_ge(T.sem["pc" + b], 1)
+            vec.wait_ge(T.sem["x" + b], 16 * (t - 1))
+            off = "off%s%d" % (b, t)
+            if t == 2:
+                v(off, ts(T["off" + b][:, :], T["X" + b][:, 0:32], 2.0 ** -25, Op.mult, 2.921875, Op.add))
+            else:
+                v(off, ts(T["off" + b][:, :], T["X" + b][:, 0:32], 0.921875, Op.add))
+            if last:
+                sub(*last, 1)
+            need(off)
+            v("gv", tt(dcol(b, t, 0, NV), T.tab[:, 0:4096].indirect(T["off" + b][:, 0:NV // 16]), T["P" + b][:, :], Op.subtract))
+            vec.wait_ge(T.sem["s" + b], t - 1)
+            sub(b, t, 0)
+            last = (b, t)
+    sub(*last, 1)
+
+    for sem in ("w47", "qoA", "qoB"):
+        vec.wait_ge(T.sem[sem], 8)
+    vec.wait_ge(T.sem.sl, 14)
+    v("w47", vec.tensor_copy(out=T.colf[:, 0:1], in_=T.psm[:, 0:1]))
+
+    def flag(b, h):
+        o = (8 if b == "A" else 72) + 32 * h
+        v("fm" + b, ts(T["fm" + b][:, 32 * h:32 * h + 32], T.psm[:, o:o + 32], -5.0, Op.is_lt, (cs(EV), cf("odd"))[h], Op.mult))
+
+    def end(b):
+        vec.wait_ge(T.sem["q" + b], 8)
+        need("w47")
+        v("t1" + b, ts(T["t1" + b][:, :], T["X" + b][:, 0:64], 4093.484375, Op.is_equal, T.colf[:, 0:1], Op.mult))
+
+    def addw(b):
+        vec.wait_ge(T.sem["wb" + b], 48)
+        need("t1" + b)
+        v("t2" + b, tt(T["t2" + b][:, :], T["W" + b][:, 0:64], T["t1" + b][:, :], Op.add))
+
+    def cutf(b):
+        need("t2" + b, "fm" + b)
+        v("t3" + b, tt(T["t3" + b][:, :], T["t2" + b][:, :], T["fm" + b][:, :], Op.mult))
+
+    def sums(b, rs):
+        need("t3" + b)
+        for r in rs:
+            out = T.rland[:, 0:8] if (b == "A" and r == 0) else T["R" + b][:, 8 * r:8 * r + 8]
+            v("kr%s%d" % (b, r), tt(out, T["t3" + b][:, r:32:4], T["t3" + b][:, 32 + r:64:4], Op.add))
+
+    flag(B0, 0)
+    end(B0)
+    flag(B0, 1)
+    addw(B0)
+    flag(B1, 0)
+    cutf(B0)
+    flag(B1, 1)
+    sums(B0, [1, 2])
+    end(B1)
+    sums(B0, [3])
+    addw(B1)
+    sums(B0, [0])
+    cutf(B1)
+    sums(B1, range(4))
+    need("krA0")
+    vec.wait_ge(T.sem.rs, 4 * 7)
+    v("s32", tt(T.s32[:, :], T.rland[:, 0:32], T.rland[:, 32:64], Op.add))
+    need("s32")
+    v("s16", tt(T.s16[:, :], T.s32[:, 0:16], T.s32[:, 16:32], Op.add))
+    need("s16")
+    v("ys", tt(T.ysum[:, :], T.s16[:, 0:8], T.s16[:, 8:16], Op.add))
 
     for h in range(2):
         q = syn if h == 0 else sca
@@ -210,38 +301,27 @@ def rank_program(g, core, T, topo):
             q.dma_start(out=T.pin[k:k + 24, :], in_=T.pts[:, 64 * h:64 * h + 64]).then_inc(T.sem.dP, 16)
     syn.dma_start(out=T.wt[:, :], in_=T.nodes[7::16, :]).then_inc(T.sem.dW, 16)
     sca.dma_start(out=T.sk[:, :], in_=T.nodes[6::16, :]).then_inc(T.sem.dS, 16)
-    sca.dma_start(out=T.n0[:, :], in_=T.nodes[:, 0:8]).then_inc(T.sem.dN, 16)
-    syn.wait_ge(T.sem.m0, 1)
-    sca.wait_ge(T.sem.m0, 1)
-
-    def load(q, gg, h):
-        a, b = (0, 1024) if h == 0 else (1024, 2047)
-        q.dma_start(out=T.basei[16 * gg:16 * gg + 7, a:b], in_=T.nodes[16 * gg:16 * gg + 7, a + 1:b + 1]).then_inc(T.sem["dB%d" % h], 16)
-    for gg in range(4):
-        load(syn, gg, 0)
-        load(sca, gg + 4, 0)
-    for a in (11, 12, 13, 14):
-        sca.dma_start(out=T.basei[a::16, 0:2047], in_=T.nodes[a::16, 1:2048]).then_inc(T.sem.dZ, 16)
-    for gg in range(4):
-        load(sca, gg + 4, 1)
-    vwait(syn, "pa1e", "pa0e", "pz")
-    for row, name in ((8, "pa1"), (9, "pa0"), (10, "pz")):
-        syn.dma_start(out=T.basei[row::16, 0:2048], in_=T[name][:, :]).then_inc(T.sem.dPc, 16)
-    for gg in range(4):
-        load(syn, gg, 1)
-    vwait(syn, "ph", "pl")
-    for row, name in ((7, "ph"), (15, "pl")):
-        syn.dma_start(out=T.basei[row::16, 0:2048], in_=T[name][:, :]).then_inc(T.sem.dPc, 16)
+    vwait(syn, "m0")
+    vwait(sca, "m0")
+    for gg in range(8):
+        q = syn if gg < 4 else sca
+        q.dma_start(out=T.basei[16 * gg:16 * gg + 13, 1024:2047], in_=T.nodes[16 * gg:16 * gg + 13, 1025:2048]).then_inc(T.sem.dU, 16)
+    syn.dma_start(out=T.n1[:, :], in_=T.nodes[:, 0:8]).then_inc(T.sem.dN, 16)
+    syn.dma_start(out=T.n0[6:128, :], in_=T.nodes[0:122, 0:8]).then_inc(T.sem.dN, 16)
+    syn.dma_start(out=T.n0[0:6, :], in_=T.nodes[8:14, 0:8]).then_inc(T.sem.dN, 16)
+    vwait(syn, "pa", "ph", "pl")
+    for k, name in ((13, "pa"), (14, "ph"), (15, "pl")):
+        syn.dma_start(out=T.basei[k::16, 0:2048], in_=T[name][:, :]).then_inc(T.sem.dPc, 16)
+    for a in range(6):
+        syn.dma_start(out=T.basei[a::16, 0:1024], in_=T.nodes[a::16, 1:1025]).then_inc(T.sem.dL, 16)
 
     fl = {"allow_small_or_imprecise_dtypes": True}
     g.iota(T.coli[:, 0:1], [[0, 1]], 0, 1).then_inc(T.sem.gi0, 1)
     g.iota(T.colp[:, 0:1], [[0, 1]], 0, -1, **fl).then_inc(T.sem.gi5, 1)
-    g.iota(T.pa1[:, :], [[1, 8], [0, 16]], 0, 8).then_inc(T.sem.gi1, 1)
-    g.iota(T.pa0[:, :], [[0, 8], [1, 16]], 1, 0).then_inc(T.sem.gi1, 1)
     g.iota(T.u1[:, :], [[1, 144]], 0, 0, **fl).then_inc(T.sem.gi3, 1)
-    g.wait_ge(T.sem.kp, 1)
-    for a in range(6):
-        g.iota(T.pat[:, a::16], [[3, 8]], a % 3, 0, **fl).then_inc(T.sem.gi2, 1)
+    g.iota(T.pa[:, :], [[2, 128]], 2, 256).then_inc(T.sem.gi1, 1)
+    vwait(g, "pat")
+    g.iota(T.pat[:, :, 0:12], [[3, 8], [0, 4], [1, 3]], 0, 0, **fl).then_inc(T.sem.gi2, 1)
 
     dire, shar = direct(core), shares(core)
     chip_mates = topo.cores_of(core)
@@ -261,14 +341,23 @@ def rank_program(g, core, T, topo):
     g.remote_dma_fused([tr(T.msg[:, :], T.land[:, 64 * slot(d, core):64 * slot(d, core) + 64], d, dir_engs[d],
                            "pa%d" % direct(d).index(core)) for d in dire], local_sem=T.sem.ls)
     g.iota(T.u2[:, :], [[1, 72], [0, 2]], 0, 0, **fl).then_inc(T.sem.gi4, 1)
+    for b in ORD:
+        vwait(g, *["kr%s%d" % (b, r) for r in range(b == "A", 4)])
+        if b == "B":
+            g.remote_dma_fused([tr(T.RB[:, 16 * i:16 * i + 16], T.rres[:, :], rel, res_engs[i], "rr") for i, (rel, _) in enumerate(shar)],
+                               local_sem=T.sem.ls)
+        else:
+            g.remote_dma_fused([tr(T.RA[:, 8 * i + 8:8 * i + 16], T.rland[:, 8 * slot(d, core) + 8:8 * slot(d, core) + 16], d, dir_engs[d], "rs")
+                                for i, d in enumerate(dire)], local_sem=T.sem.ls)
+    g.wait_ge(T.sem.ls, 12 * len(shar) + 8 * len(dire))
 
     def act(out, in_, func, sem, **kw):
         sca.activation(out=out, in_=in_, func=func, **kw).then_inc(T.sem[sem], 1)
 
     def first(b):
         sca.wait_ge(T.sem["pp" + b], 8)
-        act(T["C1" + b][:, :], T["pp" + b][:, :], Fn.Tanh, "sy" + b, bias=cf("s1"), scale=-8.0)
-        act(T["P" + b][:, :], T["pp" + b][:, :], Fn.Copy, "pc" + b)
+        act(T["C" + b][:, :], T["pp" + b][:, :], Fn.Sign, "sy" + b, bias=cf("s01"), scale=-1.0)
+        act(T["P" + b][:, :], T["pp" + b][:, 0:NV], Fn.Copy, "pc" + b)
 
     sca.wait_ge(T.sem.gi3, 1)
     sca.wait_ge(T.sem.gi5, 1)
@@ -280,54 +369,42 @@ def rank_program(g, core, T, topo):
         act(T.zt[:, 128 + 48 * k:176 + 48 * k], T.u1[:, 0:48], Fn.Abs, "ksb", bias=cf(name))
     sca.wait_ge(T.sem.ksb, 3)
     act(T.zs[:, :], T.zt[:, 128:224], Fn.Relu, "ksd", bias=1.0, scale=-1.0)
-    vwait(sca, "sg")
-    act(cs(NG), cf("sg"), Fn.Copy, "kt", scale=-1.0)
-    act(cs(SC), cf("bd"), Fn.Identity, "kt", bias=EPS, scale=2.0 - EPS)
-    act(cs(TH), cf("bd"), Fn.Identity, "kt", bias=1.0, scale=7.0)
-    act(T.colt[:, 0:1], cf("sg"), Fn.Tanh, "ku", scale=16.0)
-    act(cs(WA), cf("a"), Fn.Identity, "ku", bias=479.125 / EPS, scale=-31.875 / EPS)
-    act(cs(TA), cf("a"), Fn.Identity, "ku", bias=-10.0)
-    vwait(sca, "w7")
-    act(cs(NW), cf("w7"), Fn.Identity, "kv", bias=1.0, scale=-1.0)
-    sca.wait_ge(T.sem.ku, 3)
-    act(cs(WZ), cf("w7"), Fn.Copy, "kx", scale=cs(WA))
-    act(cs(TA), cs(TA), Fn.Abs, "kx")
-    vwait(sca, "s1")
-    sca.wait_ge(T.sem.kv, 1)
-    sca.wait_ge(T.sem.kx, 2)
+    vwait(sca, "s01")
     first("A")
-    for h in range(2):
-        sca.wait_ge(T.sem.kbase, h + 1)
-        act(T.tab[:, 2048 * h + 2:2048 * h + 2049:2], T.basef[:, 1024 * h:1024 * h + 1024], Fn.Copy, "ht")
-    for k in range(2):
-        act(T.tab[:, k:k + 1], T.basef[:, 2047:2048], Fn.Copy, "ht", scale=cs(NW))
+    vwait(sca, "basef")
+    act(T.tab[:, 2048:4096:2], T.basef[:, :], Fn.Copy, "ht")
+    act(T.tab[:, 2 * NM + 1:4096:2], T.basef[:, 0:1024].indirect(T.missl[:, NM // 16:128]), Fn.Copy, "ht", scale=below(14))
+    act(T.tab[:, 0:1], T.basef[:, 1023:1024], Fn.Copy, "ht", scale=below(14))
     first("B")
-    vwait(sca, "nu2", "nu3", "odd", "s0")
+    side = [
+        (cs(NU2), cf("u"), Fn.Identity, 0.5, -0.5),
+        (cs(WZ), row(14), Fn.Identity, row(15), 256.0),
+        (T.zt[:, 224:368], T.u2[:, :], Fn.Abs, cs(NU2), 1.0),
+        (cs(NA4), cf("a"), Fn.Identity, -7.0, -4.0),
+        (T.zp[:, :], T.zt[:, 224:368], Fn.Relu, 1.0, -1.0),
+        (cs(NU3), cf("odd"), Fn.Identity, cs(NA4), 4.0),
+        (T.zw[:, :], T.zp[:, :], Fn.Copy, 0.0, cs(WZ)),
+        (T.w0r[:, :], T.u1[:, 0:64], Fn.Identity, T.colb[:, 0:1], 0.0),
+        (T.zf[:, :], T.zp[:, :], Fn.Copy, 0.0, cf("sf")),
+        (T.zt[:, 368:512], T.u2[:, :], Fn.Abs, cs(NU3), 1.0),
+        (cs(NWH), cf("wh"), Fn.Copy, 0.0, -1.0),
+        (T.zq[:, :], T.zp[:, :], Fn.Copy, 0.0, cf("xx")),
+        (T.zh[:, :], T.zt[:, 368:512], Fn.Relu, cf("wh"), cs(NWH)),
+        (cs(EV), cf("odd"), Fn.Identity, 1.0, -1.0),
+    ]
+    sca.wait_ge(T.sem.ht, 3)
     sca.wait_ge(T.sem.gi4, 1)
-    act(T.zt[:, 224:368], T.u2[:, :], Fn.Abs, "kth", bias=cf("nu2"))
-    act(T.zt[:, 368:512], T.u2[:, :], Fn.Abs, "kth", bias=cf("nu3"))
-    act(cs(EV), cf("odd"), Fn.Identity, "kth", bias=1.0, scale=-1.0)
-    act(cs(WH), cf("odd"), Fn.Identity, "kth", bias=256.0 / EPS, scale=-255.0 / EPS)
-    act(cs(NWH), cf("odd"), Fn.Identity, "kth", bias=-256.0 / EPS, scale=255.0 / EPS)
-    act(cs(KT), cs(TA), Fn.Relu, "kth", bias=1.0, scale=-1.0)
-    sca.wait_ge(T.sem.kth, 6)
-    act(cs(QZ), cs(KT), Fn.Identity, "kzp", bias=T.colt[:, 0:1], scale=2.0 / EPS)
-    act(T.zp[:, :], T.zt[:, 224:368], Fn.Relu, "kzp", bias=1.0, scale=-1.0)
-    act(T.zh[:, :], T.zt[:, 368:512], Fn.Relu, "kzp", bias=cs(WH), scale=cs(NWH))
-    sca.wait_ge(T.sem.kzp, 3)
-    sca.wait_ge(T.sem.kt, 3)
-
-    vec.wait_ge(T.sem.kt, 3)
-    vec.wait_ge(T.sem.kv, 1)
-    need("missl")
-    vec.wait_ge(T.sem.dB0, 128)
-    vec.wait_ge(T.sem.dZ, 64)
-    vec.wait_ge(T.sem.dPc, 80)
-    ts(T.basef[:, 0:1024], T.basei[:, 0:1024], cs(SC), Op.mult, cs(NG), Op.add).then_inc(T.sem.kbase, 1)
-    vec.wait_ge(T.sem.dB1, 128)
-    ts(T.basef[:, 1024:2048], T.basei[:, 1024:2048], cs(SC), Op.mult, cs(NG), Op.add).then_inc(T.sem.kbase, 1)
-    vec.wait_ge(T.sem.kbase, 2)
-    v("tab", ts(T.tab[:, 3:4098:2], T.basef[:, 0:2048].indirect(T.missl[:, 0:128]), cs(NW), Op.mult))
+    k = 0
+    for t in range(2, V):
+        for b in ORD:
+            vwait(sca, "off%s%d" % (b, t))
+            act(T["G" + b][:, :], T.tab[:, 0:4096].indirect(T["off" + b][:, NV // 16:32]), Fn.Copy, "s" + b)
+            if k < len(side):
+                if k > 0:
+                    sca.wait_ge(T.sem.sl, k)
+                out, in_, func, bias, scale = side[k]
+                act(out, in_, func, "sl", bias=bias, scale=scale)
+                k += 1
 
     vwait(ten, "skh")
     ten.wait_ge(T.sem.ksc, 1)
@@ -353,168 +430,67 @@ def rank_program(g, core, T, topo):
 
     def tx(b, t, js):
         for j in js:
-            ten.matmul(T["X" + b][:, 0:32], T.zx[:, 15 - j:143 - j], T["C%d%s" % (t % 2, b)][:, j:512:16],
-                       j == 0, j == 15).then_inc(T.sem["x" + b], 1)
+            src = T["C" + b][:, j:512:16] if t == 1 else dcol(b, t, j, 512, 16)
+            ten.matmul(T["X" + b][:, 0:32], T.zx[:, 15 - j:143 - j], src, j == 0, j == 15).then_inc(T.sem["x" + b], 1)
 
     def pairs(out, z, src, sem, start, stop, k=128):
         for p in range(8):
-            ten.matmul(out, T[z][0:k, 14 - 2 * p:142 - 2 * p], T[src][0:k, 64 * p:64 * p + 64],
-                       start and p == 0, stop and p == 7).then_inc(T.sem[sem], 1)
+            ten.matmul(out, T[z][0:k, 14 - 2 * p:142 - 2 * p], src(p), start and p == 0, stop and p == 7).then_inc(T.sem[sem], 1)
+
+    def blocks(name, k=128):
+        return lambda p: T[name][0:k, 64 * p:64 * p + 64]
+
+    def visit(b, t):
+        return lambda p: dcol(b, t, 64 * p, 64 * p + 64)
 
     nd, nx = len(dire), len(cross(core))
     vwait(ten, "lp0", "lp1", "msg")
     spread("A", [("msg", 0, None)] + [("land", 64 * i, "pa%d" % i) for i in range(nd)])
+    vwait(ten, "zx")
+    ten.wait_ge(T.sem.syA, 1)
+    tx("A", 1, range(16))
     vwait(ten, "missl")
     spread("B", [("land", 64 * (nd + i), "pb%d" % i) for i in range(nx)])
-    vwait(ten, "zx")
-    for b in "AB":
-        ten.wait_ge(T.sem["sy" + b], 1)
-        tx(b, 1, range(16))
-
-    def swait(q, b, t):
-        if t > 2 or b == B1:
-            q.wait_ge(T.sem["s" + b], t - 1 if b == B1 else t - 2)
-
+    ten.wait_ge(T.sem.syB, 1)
+    tx("B", 1, range(16))
     for t in range(2, V):
         for b in ORD:
-            W, c = T["W" + b][:, 0:64], "C%d%s" % (t % 2, b)
-            ten.wait_ge(T.sem["c" + b], t - 1)
+            W = T["W" + b][:, 0:64]
             if t < V - 1:
-                tx(b, t, range(0, 16, 2))
-            swait(ten, b, t)
-            if t < V - 1:
-                tx(b, t, range(1, 16, 2))
-            if t == 5 and b == B0:
-                ten.wait_ge(T.sem.kzw, 4)
-                for p in range(8):
-                    ten.matmul(T.psm[:, 0:2], T.zw[:, 14 - 2 * p:142 - 2 * p], T.colb[:, 0:2], p == 0, p == 7).then_inc(T.sem.w47, 1)
+                for e in range(2):
+                    vwait(ten, "sub%d%s%d" % (e, b, t))
+                    tx(b, t, range(e, 16, 2))
+            if t == 6 and b == B1:
+                ten.wait_ge(T.sem.sl, 8)
+                pairs(T.psm[:, 0:1], "zw", lambda p: T.colb[:, 1:2], "w47", True, True)
+            if t == 7:
+                pairs(W, "zw", lambda p: T.w0r[:, :], "wb" + b, True, False)
             if t == 8:
-                ten.wait_ge(T.sem["f" + b], 4)
+                ten.wait_ge(T.sem.sl, 9)
                 o = 8 if b == "A" else 72
-                pairs(T.psm[:, o:o + 64], "zq", "F" + b, "qo" + b, True, True)
+                pairs(T.psm[:, o:o + 64], "zf", blocks("C" + b), "qo" + b, True, True)
             if t == 11:
-                ten.wait_ge(T.sem["hx" + b], 64)
-                ten.wait_ge(T.sem["hy" + b], 64)
-                pairs(W, "zh", "h1" + b, "wb" + b, True, False)
+                ten.wait_ge(T.sem.sl, 13)
+                ten.wait_ge(T.sem["hx" + b], 128)
+                pairs(W, "zh", blocks("h1" + b), "wb" + b, False, False)
             if t == 12:
-                pairs(W, "zw", c, "wa" + b, False, False)
+                pairs(W, "zw", visit(b, t), "wb" + b, False, False)
             if t == 13:
-                pairs(W, "zw", c, "wb" + b, False, False)
-                ten.wait_ge(T.sem["hz" + b], 16)
-                ten.wait_ge(T.sem["hw" + b], 16)
-                pairs(W, "zh", "h2" + b, "wb" + b, False, False, 16 * len(H2))
+                ten.wait_ge(T.sem["hz" + b], 32)
+                pairs(W, "zh", blocks("h2" + b, 32), "wb" + b, False, False, 32)
             if t == V - 1:
-                pairs(T["X" + b][:, 0:64], "zq", c, "q" + b, True, True)
-                pairs(W, "zw", c, "wb" + b, False, True)
+                pairs(W, "zw", visit(b, t - 1), "wb" + b, False, False)
+                vwait(ten, "sub1%s%d" % (b, t))
+                pairs(T["X" + b][:, 0:64], "zq", visit(b, t), "q" + b, True, True)
+                pairs(W, "zw", visit(b, t), "wb" + b, False, True)
 
-    for t in list(H1) + list(H2):
+    for t in range(2, 12, 2):
         for b in ORD:
-            syn.wait_ge(T.sem["c" + b], t - 1)
-            swait(syn, b, t)
-            dst, k, sem = ("h1", t - H1[0], "hx" if t % 2 == 0 else "hy") if t in H1 else ("h2", t - H2[0], "hz" if t % 2 == 0 else "hw")
-            syn.dma_start(out=T[dst + b][16 * k:16 * k + 16, :], in_=T["C%d%s" % (t % 2, b)][7::8, :]).then_inc(T.sem[sem + b], 16)
-
-    def clamp(b, t):
-        n = 1 if t == 2 and b == B0 else 2
-        vec.wait_ge(T.sem["g" + b], t - 1)
-        ts(T["C%d%s" % (t % 2, b)][:, 0:512:n], T["D" + b][:, 0:512:n], 1.0, Op.min, -1.0, Op.max).then_inc(T.sem["c" + b], 1)
-
-    vec.wait_ge(T.sem.ht, 4)
-    need("tab")
-    last = None
-    for t in range(2, V):
-        for b in ORD:
-            D, C = T["D" + b], T["C%d%s" % (t % 2, b)]
-            if t == 2:
-                vec.wait_ge(T.sem["pc" + b], 1)
-            vec.wait_ge(T.sem["x" + b], 16 * (t - 1))
-            ts(T["off" + b][:, :], T["X" + b][:, 0:32], 2.953125 if t > 2 else 4.953125, Op.add).then_inc(T.sem["o" + b], 1)
-            if last:
-                clamp(*last)
-            if t - 2 in H1:
-                vec.wait_ge(T.sem[("hx" if t % 2 == 0 else "hy") + b], 16 * ((t - 2) // 2))
-            elif t - 2 in H2:
-                vec.wait_ge(T.sem[("hz" if t % 2 == 0 else "hw") + b], 16)
-            elif t == 14:
-                vec.wait_ge(T.sem["wa" + b], 8)
-            vec.wait_ge(T.sem["o" + b], t - 1)
-            tt(D[:, :], T.tab[:, 0:4098].indirect(T["off" + b][:, 0:32]), T["P" + b][:, :], Op.subtract).then_inc(T.sem["g" + b], 1)
-            last = (b, t)
-            if t > 2 or b != B0:
-                sca.wait_ge(T.sem["g" + b], t - 1)
-                act(C[:, 1:512:2], D[:, 1:512:2], Fn.Tanh, "s" + b, scale=cs(TH))
-            if t == 3 and b == B0:
-                for k, cc in ((0, 2047), (1, 0)):
-                    act(T.colb[:, k:k + 1], T.basef[:, cc:cc + 1], Fn.Copy, "kzw")
-                act(T.zw[:, :], T.zp[:, :], Fn.Copy, "kzw", scale=cs(WZ))
-            if t == 3 and b == B1:
-                act(T.zq[:, :], T.zp[:, :], Fn.Copy, "kzw", scale=cs(QZ))
-            if 4 <= t < 8:
-                a = 128 * (t - 4)
-                act(T["F" + b][:, a:a + 128], T["pp" + b][:, a:a + 128], Fn.Tanh, "f" + b, bias=cf("s0"), scale=-8.0)
-
-    for sem in ("w47", "qoA", "qoB"):
-        vec.wait_ge(T.sem[sem], 8)
-    v("w07", vec.tensor_copy(out=T.colf[:, 0:2], in_=T.psm[:, 0:2]))
-    clamp(*last)
-
-    def flag(b, h):
-        o = (8 if b == "A" else 72) + 32 * h
-        v("fm" + b, ts(T["fm" + b][:, 32 * h:32 * h + 32], T.psm[:, o:o + 32], -5.0, Op.is_lt, (cs(EV), cf("odd"))[h], Op.mult))
-
-    def end(b):
-        vec.wait_ge(T.sem["q" + b], 8)
-        need("w07")
-        v("t1" + b, ts(T["t1" + b][:, :], T["X" + b][:, 0:64], -5.0, Op.is_lt, T.colf[:, 0:1], Op.mult))
-
-    def add0(b):
-        need("t1" + b)
-        v("t4" + b, ts(T["t4" + b][:, :], T["t1" + b][:, :], T.colf[:, 1:2], Op.add))
-
-    def addw(b):
-        vec.wait_ge(T.sem["wb" + b], 32)
-        need("t4" + b)
-        v("t2" + b, tt(T["t2" + b][:, :], T["W" + b][:, 0:64], T["t4" + b][:, :], Op.add))
-
-    def cutf(b):
-        need("t2" + b, "fm" + b)
-        v("t3" + b, tt(T["t3" + b][:, :], T["t2" + b][:, :], T["fm" + b][:, :], Op.mult))
-
-    def sums(b):
-        need("t3" + b)
-        for r in range(4):
-            out = T.rland[:, 0:8] if (b == "A" and r == 0) else T["R" + b][:, 8 * r:8 * r + 8]
-            tt(out, T["t3" + b][:, r:32:4], T["t3" + b][:, 32 + r:64:4], Op.add).then_inc(T.sem["kr" + b], 1)
-
-    vec.wait_ge(T.sem.kth, 6)
-    flag("B", 0)
-    end("B")
-    flag("B", 1)
-    add0("B")
-    flag("A", 0)
-    addw("B")
-    flag("A", 1)
-    cutf("B")
-    end("A")
-    sums("B")
-    add0("A")
-    addw("A")
-    cutf("A")
-    sums("A")
-    g.wait_ge(T.sem.krB, 4)
-    g.remote_dma_fused([tr(T.RB[:, 16 * i:16 * i + 16], T.rres[:, :], rel, res_engs[i], "rr") for i, (rel, _) in enumerate(shar)],
-                       local_sem=T.sem.ls)
-    g.wait_ge(T.sem.krA, 4)
-    g.remote_dma_fused([tr(T.RA[:, 8 * i + 8:8 * i + 16], T.rland[:, 8 * slot(d, core) + 8:8 * slot(d, core) + 16], d, dir_engs[d], "rs")
-                        for i, d in enumerate(dire)], local_sem=T.sem.ls)
-    vec.wait_ge(T.sem.krA, 4)
-    vec.wait_ge(T.sem.rs, 4 * 7)
-    v("s32", tt(T.s32[:, :], T.rland[:, 0:32], T.rland[:, 32:64], Op.add))
-    need("s32")
-    v("s16", tt(T.s16[:, :], T.s32[:, 0:16], T.s32[:, 16:32], Op.add))
-    need("s16")
-    tt(T.ysum[:, :], T.s16[:, 0:8], T.s16[:, 8:16], Op.add).then_inc(T.sem.ys, 1)
-    syn.wait_ge(T.sem.ys, 1)
+            vwait(syn, "sub1%s%d" % (b, t + 1))
+            dst, k, sem = ("h1", 16 * (t - 2), "hx") if t < 10 else ("h2", 0, "hz")
+            for e in range(2):
+                syn.dma_start(out=T[dst + b][k + 16 * e:k + 16 * e + 16, :],
+                              in_=T["D" + b][14 + e::16, 512 * (t - 2):512 * t]).then_inc(T.sem[sem + b], 16)
+    vwait(syn, "ys")
     syn.dma_start(out=T.y[:, :], in_=T.ysum[:, :]).then_inc(T.sem.dY, 16)
     syn.wait_ge(T.sem.dY, 16)
-    g.wait_ge(T.sem.ls, 12 * len(shar) + 8 * nd)

@@ -4,47 +4,42 @@ from concourse.mybir import AluOpType as Op, ActivationFunctionType as Fn
 V = 15
 ORD = "AB"
 B0, B1 = ORD
-NV = 288
-NM = 1280
+NV = 352
+NM = 1472
+RE, RS = 4, 8
 U = 2.0 ** -46
 KV = 11.0 * 2 ** 18
 SCRATCH = {
     "pin": ("sbuf", [128, 64], "int32"), "pq": ("sbuf", [128, 64], "int32"), "msg": ("sbuf", [128, 64], "float16"),
-    "land": ("sbuf", [128, 448], "float16"), "rmsg": ("sbuf", [128, 64], "float16"), "rres": ("sbuf", [128, 16], "float32"),
+    "land": ("sbuf", [128, 448], "float16"), "rmsg": ("sbuf", [128, 64], "float16"), "rres": ("sbuf", [128, 32], "float32"),
     "coli": ("sbuf", [128, 16], "int32"), "colf": ("sbuf", [128, 64], "float32"), "colb": ("sbuf", [128, 8], "bfloat16"),
-    "colp": ("sbuf", [128, 8], "float32"), "cols": ("sbuf", [128, 16], "float32"),
+    "colp": ("sbuf", [128, 8], "float32"), "cols": ("sbuf", [128, 32], "float32"),
     "pat": ("sbuf", [128, 8, 16], "float32"), "lt": ("sbuf", [128, 16], "float32"), "eq": ("sbuf", [128, 16], "float32"),
     "u1": ("sbuf", [128, 144], "float32"), "u2": ("sbuf", [128, 144], "float32"),
-    "lp": ("sbuf", [128, 256], "bfloat16"),
-    "skh": ("sbuf", [128, 128], "float16"), "idn": ("sbuf", [128, 128], "bfloat16"), "skt": ("sbuf", [128, 128], "float16"),
-    "zs": ("sbuf", [128, 96], "bfloat16"), "zt": ("sbuf", [128, 512], "float32"),
-    "zx": ("sbuf", [128, 144], "bfloat16"), "zw": ("sbuf", [128, 144], "bfloat16"), "zf": ("sbuf", [128, 144], "bfloat16"),
+    "lp": ("sbuf", [128, 256], "bfloat16"), "zt": ("sbuf", [128, 544], "float32"),
+    "zx": ("sbuf", [128, 144], "bfloat16"), "zw": ("sbuf", [128, 144], "bfloat16"),
     "zq": ("sbuf", [128, 144], "bfloat16"), "zh": ("sbuf", [128, 144], "bfloat16"), "zp": ("sbuf", [128, 144], "bfloat16"),
-    "w0r": ("sbuf", [128, 64], "bfloat16"),
-    "sk": ("sbuf", [128, 128], "int32"), "wt": ("sbuf", [128, 128], "int32"),
-    "n0": ("sbuf", [128, 8], "int32"), "n1": ("sbuf", [128, 8], "int32"),
+    "sk": ("sbuf", [128, 2, 64], "int32"), "skf": ("sbuf", [128, 2, 64], "float32"), "skw": ("sbuf", [128, 128], "float32"),
+    "wt": ("sbuf", [128, 128], "int32"), "n0": ("sbuf", [128, 8], "int32"),
     "pa": ("sbuf", [128, 128], "int32"), "ph": ("sbuf", [128, 128], "int32"), "pl": ("sbuf", [128, 128], "int32"),
     "missl": ("sbuf", [128, 128], "uint16"),
     "basei": ("sbuf", [128, 2048], "int32"), "basef": ("sbuf", [128, 1024], "float32"),
     "tab": ("sbuf", [128, 4096], "float32"),
-    "rland": ("sbuf", [128, 64], "float32"), "s32": ("sbuf", [128, 32], "float32"), "s16": ("sbuf", [128, 16], "float32"),
-    "ysum": ("sbuf", [128, 8], "float32"),
-    "psm": ("psum", [128, 144], "float32"),
+    "rland": ("sbuf", [128, 176], "float32"), "RB": ("sbuf", [128, 64], "float32"),
+    "s64": ("sbuf", [128, 64], "float32"), "s32": ("sbuf", [128, 32], "float32"), "ysum": ("sbuf", [128, 16], "float32"),
+    "psm": ("psum", [128, 8], "float32"),
 }
-SEMAPHORES = ["vc", "gi0", "gi1", "gi2", "gi3", "gi4", "gi5", "dP", "dS", "dW", "dN", "dU", "dL", "dPc", "dY",
-              "ksb", "ksc", "ksd", "ht", "w47", "lt", "ll", "sl",
-              "pa0", "pa1", "pa2", "pb0", "pb1", "pb2", "pb3", "rs", "rm", "rr", "ls", "rl"]
+SEMAPHORES = ["vc", "ac", "gi0", "gi1", "gi2", "gi3", "gi4", "gi5", "dP", "dS", "dW", "dN", "dU", "dL", "dPc", "dY",
+              "ht", "w47", "sl", "pa0", "pa1", "pa2", "pb0", "pb1", "pb2", "pb3", "rs", "rm", "rr", "ls", "rl"]
 for _b in "AB":
     SCRATCH.update({
         "off" + _b: ("sbuf", [128, 32], "uint16"), "P" + _b: ("sbuf", [128, NV], "float32"), "G" + _b: ("sbuf", [128, 512 - NV], "float32"),
         "D" + _b: ("sbuf", [128, 512 * (V - 2)], "float16"), "C" + _b: ("sbuf", [128, 512], "bfloat16"),
         "h1" + _b: ("sbuf", [128, 512], "float16"), "h2" + _b: ("sbuf", [128, 512], "float16"),
-        "R" + _b: ("sbuf", [128, 32], "float32"), "fm" + _b: ("sbuf", [128, 64], "float32"), "t1" + _b: ("sbuf", [128, 64], "float32"),
-        "t2" + _b: ("sbuf", [128, 64], "float32"), "t3" + _b: ("sbuf", [128, 64], "float32"),
-        "pp" + _b: ("psum", [128, 512], "float32"), "X" + _b: ("psum", [128, 64], "float32"), "W" + _b: ("psum", [128, 64], "float32"),
+        "t1" + _b: ("sbuf", [128, 64], "float32"),
+        "pp" + _b: ("psum", [128, 32, 16], "float32"), "X" + _b: ("psum", [128, 64], "float32"), "W" + _b: ("psum", [128, 64], "float32"),
     })
-    SEMAPHORES += [k + _b for k in ("pp", "pc", "sy", "s", "x", "wb", "qo", "q", "hx", "hz")]
-NU2, WZ, NA4, NU3, NWH, EV = range(6)
+    SEMAPHORES += [k + _b for k in ("pp", "pc", "sy", "s", "x", "wb", "q", "hx", "hz")]
 
 
 def mask_of(engs):
@@ -72,6 +67,9 @@ def rank_program(g, core, T, topo):
     def slot(dst, src):
         return (direct(dst) + cross(dst)).index(src)
 
+    def home(dst, src):
+        return T.rland[:, 16 * slot(dst, src) + 64:16 * slot(dst, src) + 80]
+
     def tr(src_ap, dst_ap, dst, engs, sem):
         rid, pid = topo.addr(dst, core)
         return RemoteDMATransfer(dst_ids=[DstId(rid=rid, pnc=pid)], dma_engine_mask=mask_of(engs), remote_sem=T.sem[sem],
@@ -83,12 +81,12 @@ def rank_program(g, core, T, topo):
                 if rel != core:
                     continue
                 engs = [topo.engines(core, d)[4 * i:4 * i + 4] for i, d in enumerate(dests)]
-                g.wait_ge(T.sem.rm, 4)
+                g.wait_ge(T.sem.rm, RE)
                 g.remote_dma_fused([tr(T.rmsg[:, :], T.land[:, 64 * slot(d, c):64 * slot(d, c) + 64], d, engs[i],
                                        "pb%d" % cross(d).index(c)) for i, d in enumerate(dests)], local_sem=T.sem.rl)
-                g.wait_ge(T.sem.rr, 8)
-                g.remote_dma_fused([tr(T.rres[:, 8 * i:8 * i + 8], T.rland[:, 8 * slot(d, c) + 8:8 * slot(d, c) + 16], d, engs[i], "rs")
-                                    for i, d in enumerate(dests)], local_sem=T.sem.rl)
+                g.wait_ge(T.sem.rr, RS)
+                g.remote_dma_fused([tr(T.rres[:, 16 * i:16 * i + 16], home(d, c), d, engs[i], "rs") for i, d in enumerate(dests)],
+                                   local_sem=T.sem.rl)
                 g.wait_ge(T.sem.rl, 16)
         return
 
@@ -117,17 +115,18 @@ def rank_program(g, core, T, topo):
     def tt(out, a, b, op):
         return vec.tensor_tensor(out=out, in0=a, in1=b, op=op)
 
-    col = {}
+    col, scol = {}, {}
 
     def cf(name):
         k = col.setdefault(name, len(col) + 1)
         return T.colf[:, k:k + 1]
 
+    def cs(name):
+        k = scol.setdefault(name, len(scol))
+        return T.cols[:, k:k + 1]
+
     def ci(k):
         return T.coli[:, k:k + 1]
-
-    def cs(k):
-        return T.cols[:, k:k + 1]
 
     def below(k):
         return T.lt[:, k:k + 1]
@@ -138,6 +137,29 @@ def rank_program(g, core, T, topo):
     def dcol(b, t, a=0, z=512, s=1):
         return T["D" + b][:, 512 * (t - 2) + a:512 * (t - 2) + z:s]
 
+    minus_p = T.colp[:, 0:1]
+    early = [
+        (cs("hi"), minus_p, Fn.Sign, -78.5, -1.0, 0),
+        (cs("w"), cs("hi"), Fn.Identity, 512.5 * U, -511.5 * U, 1),
+        (cs("k0"), cs("hi"), Fn.Identity, minus_p, 32.0, 1),
+        (cs("nw"), cs("hi"), Fn.Identity, -512.5 * U, 511.5 * U, 1),
+        (cs("k1"), cs("k0"), Fn.Identity, 1.0, 1.0, 3),
+        (T.zt[:, 0:128], T.pat[:, :, :], Fn.Abs, cs("k0"), 1.0, 3),
+        (T.zt[:, 128:256], T.pat[:, :, :], Fn.Abs, cs("k1"), 1.0, 5),
+        (T.lp[:, :], T.zt[:, 0:256], Fn.Relu, cs("w"), cs("nw"), 7),
+        (cs("n6"), below(6), Fn.Copy, 0.0, -1.0, 7),
+        (cs("c0"), below(12), Fn.Copy, 0.0, U, 7),
+        (cs("sg"), below(3), Fn.Identity, cs("n6"), 2.0, 9),
+        (cs("sa"), below(9), Fn.Identity, cs("n6"), 2.0, 9),
+        (cs("xa"), cs("sg"), Fn.Identity, row(13), KV, 11),
+        (cs("sh"), cs("sg"), Fn.Copy, 0.0, -U / 2, 11),
+        (cs("sf"), below(12), Fn.Identity, cs("sa"), -1.0, 12),
+        (cs("wr"), row(14), Fn.Identity, row(15), 1.0, 12),
+        (cs("sb"), cs("sf"), Fn.Identity, cs("sh"), -U / 2, 15),
+        (cs("xx"), cs("sf"), Fn.Identity, cs("xa"), -32 * KV, 15),
+    ]
+    COLS, LP = len(early), 8
+
     def cv(name, in0, *args, deps=()):
         if deps:
             need(*deps)
@@ -146,11 +168,13 @@ def rank_program(g, core, T, topo):
     def iv(k, *args):
         v("i%d" % k, ts(ci(k), ci(0), *args))
 
-    v("m0", vec.memset(T.basei[:, 2040:2048], 0))
-    v("pq", vec.memset(T.pq[:, :], 0))
+    v("m0", vec.memset(T.basei[:, 1024:2048], 0))
     v("pat", vec.memset(T.pat[:, :, :], -99.0))
+    v("pq", vec.memset(T.pq[:, :], 0))
     v("m1", vec.memset(T.basei[:, 0:1024], 0))
-    vec.wait_ge(T.sem.dP, 64)
+    vec.wait_ge(T.sem.gi1, 1)
+    v("pa", ts(T.pa[:, :], T.pa[:, :], 4095, Op.bitwise_and))
+    vec.wait_ge(T.sem.dP, 32)
     need("pq")
     v("q0", ts(T.pq[0:48, :], T.pin[0:48, :], 10, Op.arith_shift_right))
     v("q1", ts(T.pq[64:112, :], T.pin[64:112, :], 1023, Op.bitwise_and))
@@ -158,68 +182,53 @@ def rank_program(g, core, T, topo):
     iv(1, 15, Op.bitwise_and)
     need("q0", "q1")
     v("msg", vec.tensor_copy(out=T.msg[:, :], in_=T.pq[:, :]))
-    iv(8, 4, Op.arith_shift_right, 1, Op.bitwise_and)
-    cv("na", ci(1), -1.0, Op.mult, -16.0, Op.add, deps=["i1"])
-    cv("nb", ci(1), -1.0, Op.mult, -1016.0, Op.add)
-    vec.wait_ge(T.sem.dS, 16)
-    v("skh", ts(T.skh[:, :], T.sk[:, :], -1.0, Op.add))
-    cv("ne", ci(8), -1000.0, Op.mult, cf("na"), Op.add, deps=["i8", "na"])
-    cv("no", ci(8), 1000.0, Op.mult, cf("nb"), Op.add, deps=["nb"])
-    vec.wait_ge(T.sem.gi1, 1)
-    v("pa", ts(T.pa[:, :], T.pa[:, :], 4095, Op.bitwise_and))
     vec.wait_ge(T.sem.dW, 16)
     v("ph", ts(T.ph[:, :], T.wt[:, :], 8, Op.arith_shift_right))
     v("pl", ts(T.pl[:, :], T.wt[:, :], 255, Op.bitwise_and))
-    cv("a", ci(1), 1.0, Op.mult)
-    iv(3, 63, Op.bitwise_and)
-    iv(6, 6, Op.arith_shift_right)
+    cv("a", ci(1), 1.0, Op.mult, deps=["i1"])
+    v("n0", vec.memset(T.n0[:, :], 0))
     vec.wait_ge(T.sem.gi3, 1)
     need("a")
     v("lt", ts(T.lt[:, :], T.u1[:, 0:16], cf("a"), Op.is_gt))
     v("eq", ts(T.eq[:, :], T.u1[:, 0:16], cf("a"), Op.is_equal))
-    cv("p63", ci(3), 1.0, Op.mult, deps=["i3"])
-    cv("p24", ci(3), -24.0, Op.add)
-    cv("w", ci(6), U - 1024 * U, Op.mult, 1024 * U, Op.add, deps=["i6"])
-    cv("sg", below(3), 2.0, Op.mult, below(6), Op.subtract, deps=["lt"])
-    vec.wait_ge(T.sem.lt, 1)
-    v("skt", vec.tensor_copy(out=T.skt[:, :], in_=T.ppB[:, 0:128]))
-    vec.wait_ge(T.sem.gi2, 1)
-    need("w")
-    v("lp0", ts(T.lp[:, 0:128], T.pat[:, :, :], cf("p63"), Op.is_equal, cf("w"), Op.mult))
-    v("lp1", ts(T.lp[:, 128:256], T.pat[:, :, :], cf("p24"), Op.is_equal, cf("w"), Op.mult))
+    vec.wait_ge(T.sem.dS, 32)
+    v("skf", ts(T.skf[:, :, :], T.sk[:, :, :], -1.0, Op.add))
     cv("sm", below(6), U, Op.mult, row(13), Op.add, deps=["eq"])
     cv("g0", below(6), 2.0 ** -25 + U / 2, Op.mult)
-    cv("sa", below(9), 2.0, Op.mult, below(6), Op.subtract)
-    cv("c0", below(12), U, Op.mult)
-    cv("sc", cf("sm"), row(14), Op.add, row(15), Op.add, deps=["sm"])
-    cv("ng", below(3), -U, Op.mult, cf("g0"), Op.add, deps=["g0"])
-    cv("sf", cf("sa"), below(12), Op.subtract, deps=["sa"])
-    cv("xx", cf("sg"), KV, Op.mult, row(13), Op.add)
+    need("skf")
+    for b in range(4):
+        v("skw", vec.transpose(out=T.skw[:, b:128:4], in_=T.skf[:, :, 16 * b:16 * b + 16]))
+    cv("sc", cf("sm"), row(14), Op.add, row(15), Op.add, deps=["g0"])
+    cv("ng", below(3), -U, Op.mult, cf("g0"), Op.add)
+    need("skw")
+    v("ml0", vec.tensor_copy(out=T.missl[:, 0:64], in_=T.skw[:, 0:64]))
+    v("missl", ts(T.missl[:, 64:128], T.skw[:, 64:128], -1024.0, Op.add))
     cv("u", ci(0), cf("a"), Op.subtract, 15.0, Op.add)
-    cv("sb", cf("sg"), cf("sf"), Op.add, -U / 2, Op.mult, deps=["sf"])
-    iv(4, 1, Op.bitwise_and)
-    need("u")
-    v("zx", ts(T.zx[:, :], T.u1[:, 0:144], cf("u"), Op.is_equal, cf("xx"), Op.mult))
-    vec.wait_ge(T.sem.dN, 48)
-    cv("s1", T.n1[:, 1:2], cf("sm"), Op.mult, cf("sb"), Op.add, deps=["sb"])
-    cv("odd", ci(4), 1.0, Op.mult, deps=["i4"])
-    cv("wh", ci(8), -255.0, Op.mult, 256.0, Op.add)
-    cv("s01", T.n0[:, 0:1], cf("c0"), Op.mult, cf("s1"), Op.add, deps=["s1"])
-    vec.wait_ge(T.sem.ll, 64)
-    v("ml0", vec.tensor_copy(out=T.missl[:, 0:NM // 16], in_=T.ppB[:, 128:128 + NM // 16]))
-    v("missl", ts(T.missl[:, NM // 16:128], T.ppB[:, 128 + NM // 16:256], -1024.0, Op.add))
 
-    vec.wait_ge(T.sem.dU, 128)
+    vec.wait_ge(T.sem.dU, 96)
     vec.wait_ge(T.sem.dPc, 48)
-    v("basef", ts(T.basef[:, :], T.basei[:, 1024:2048], cf("sc"), Op.mult, cf("ng"), Op.add))
-    vec.wait_ge(T.sem.dL, 96)
-    v("hitL", ts(T.tab[:, 2:2048:2], T.basei[:, 1:1024], cf("sc"), Op.mult, cf("ng"), Op.add))
     need("missl")
-    v("tab", ts(T.tab[:, 1:2 * NM:2], T.basei[:, 0:2048].indirect(T.missl[:, 0:NM // 16]), cf("sm"), Op.mult, cf("ng"), Op.add))
-    v("colb", vec.tensor_copy(out=T.colb[:, 0:2], in_=T.basei[:, 0:2048:2047]))
+    v("basef", ts(T.basef[:, :], T.basei[:, 1024:2048], cf("sc"), Op.mult, cf("ng"), Op.add))
+    v("missU", ts(T.tab[:, 2049:2 * NM:2], T.basei[:, 1024:2048].indirect(T.missl[:, 64:NM // 16]), cf("sm"), Op.mult, cf("ng"), Op.add))
+    vec.wait_ge(T.sem.ac, COLS)
+    need("u")
+    v("zx", ts(T.zx[:, :], T.u1[:, 0:144], cf("u"), Op.is_equal, cs("xx"), Op.mult))
+    vec.wait_ge(T.sem.dL, 96)
+    cv("s1", T.basei[:, 0:1], cf("sm"), Op.mult, cs("sb"), Op.add)
+    vec.wait_ge(T.sem.dN, 16)
+    cv("s01", T.n0[:, 0:1], cs("c0"), Op.mult, cf("s1"), Op.add, deps=["s1"])
+    cv("w0", T.basei[:, 0:1], cs("wr"), Op.mult)
+    v("hitL", ts(T.tab[:, 2:2048:2], T.basei[:, 1:1024], cf("sc"), Op.mult, cf("ng"), Op.add))
+    v("tab", ts(T.tab[:, 1:2048:2], T.basei[:, 0:2048].indirect(T.missl[:, 0:64]), cf("sm"), Op.mult, cf("ng"), Op.add))
+    iv(4, 1, Op.bitwise_and)
+    iv(8, 4, Op.arith_shift_right, 1, Op.bitwise_and)
+    v("colb", vec.tensor_copy(out=T.colb[:, 0:1], in_=T.basei[:, 2047:2048]))
+    cv("odd", ci(4), 1.0, Op.mult, deps=["i4"])
+    v("tab", ts(T.tab[:, 2:4], T.tab[:, 2:4], cf("w0"), Op.add))
+    cv("wh", ci(8), -255.0, Op.mult, 256.0, Op.add, deps=["i8"])
 
     def sub(b, t, e):
-        v("sub%d%s%d" % (e, b, t), tt(dcol(b, t, NV + e, 512, 2), T["G" + b][:, e:512 - NV:2], T["pp" + b][:, NV + e:512:2], Op.subtract))
+        v("sub%d%s%d" % (e, b, t), tt(dcol(b, t, NV + e, 512, 2), T["G" + b][:, e:512 - NV:2], T["pp" + b][:, NV // 16:32, e:16:2], Op.subtract))
 
     vec.wait_ge(T.sem.ht, 3)
     need("tab")
@@ -231,7 +240,7 @@ def rank_program(g, core, T, topo):
             vec.wait_ge(T.sem["x" + b], 16 * (t - 1))
             off = "off%s%d" % (b, t)
             if t == 2:
-                v(off, ts(T["off" + b][:, :], T["X" + b][:, 0:32], 2.0 ** -25, Op.mult, 2.921875, Op.add))
+                v(off, ts(T["off" + b][:, :], T["X" + b][:, 0:32], 2.0 ** -25, Op.mult, 2.921875 - 16.5, Op.add))
             else:
                 v(off, ts(T["off" + b][:, :], T["X" + b][:, 0:32], 0.921875, Op.add))
             if last:
@@ -242,94 +251,59 @@ def rank_program(g, core, T, topo):
             sub(b, t, 0)
             last = (b, t)
     sub(*last, 1)
-
-    for sem in ("w47", "qoA", "qoB"):
-        vec.wait_ge(T.sem[sem], 8)
-    vec.wait_ge(T.sem.sl, 14)
+    vec.wait_ge(T.sem.w47, 8)
     v("w47", vec.tensor_copy(out=T.colf[:, 0:1], in_=T.psm[:, 0:1]))
 
-    def flag(b, h):
-        o = (8 if b == "A" else 72) + 32 * h
-        v("fm" + b, ts(T["fm" + b][:, 32 * h:32 * h + 32], T.psm[:, o:o + 32], -5.0, Op.is_lt, (cs(EV), cf("odd"))[h], Op.mult))
-
-    def end(b):
+    for b in ORD:
         vec.wait_ge(T.sem["q" + b], 8)
         need("w47")
-        v("t1" + b, ts(T["t1" + b][:, :], T["X" + b][:, 0:64], 4093.484375, Op.is_equal, T.colf[:, 0:1], Op.mult))
-
-    def addw(b):
-        vec.wait_ge(T.sem["wb" + b], 48)
-        need("t1" + b)
-        v("t2" + b, tt(T["t2" + b][:, :], T["W" + b][:, 0:64], T["t1" + b][:, :], Op.add))
-
-    def cutf(b):
-        need("t2" + b, "fm" + b)
-        v("t3" + b, tt(T["t3" + b][:, :], T["t2" + b][:, :], T["fm" + b][:, :], Op.mult))
-
-    def sums(b, rs):
-        need("t3" + b)
-        for r in rs:
-            out = T.rland[:, 0:8] if (b == "A" and r == 0) else T["R" + b][:, 8 * r:8 * r + 8]
-            v("kr%s%d" % (b, r), tt(out, T["t3" + b][:, r:32:4], T["t3" + b][:, 32 + r:64:4], Op.add))
-
-    flag(B0, 0)
-    end(B0)
-    flag(B0, 1)
-    addw(B0)
-    flag(B1, 0)
-    cutf(B0)
-    flag(B1, 1)
-    sums(B0, [1, 2])
-    end(B1)
-    sums(B0, [3])
-    addw(B1)
-    sums(B0, [0])
-    cutf(B1)
-    sums(B1, range(4))
-    need("krA0")
+        v("t1", ts(T["t1" + b][:, :], T["X" + b][:, 0:64], 4093.484375, Op.is_equal, T.colf[:, 0:1], Op.mult))
+        vec.wait_ge(T.sem["wb" + b], 40)
+        need("t1")
+        v("kr" + b, tt(T.rland[:, 0:64] if b == "A" else T.RB[:, :], T["W" + b][:, 0:64], T["t1" + b][:, :], Op.add))
+    need("krA")
     vec.wait_ge(T.sem.rs, 4 * 7)
-    v("s32", tt(T.s32[:, :], T.rland[:, 0:32], T.rland[:, 32:64], Op.add))
+    v("s64", tt(T.s64[:, :], T.rland[:, 48:112], T.rland[:, 112:176], Op.add))
+    need("s64")
+    v("s32", tt(T.s32[:, :], T.s64[:, 0:32], T.s64[:, 32:64], Op.add))
     need("s32")
-    v("s16", tt(T.s16[:, :], T.s32[:, 0:16], T.s32[:, 16:32], Op.add))
-    need("s16")
-    v("ys", tt(T.ysum[:, :], T.s16[:, 0:8], T.s16[:, 8:16], Op.add))
+    v("ys", tt(T.ysum[:, :], T.s32[:, 0:16], T.s32[:, 16:32], Op.add))
 
-    for h in range(2):
-        q = syn if h == 0 else sca
-        for lo in range(2):
-            k = 64 * lo + 24 * h
-            q.dma_start(out=T.pin[k:k + 24, :], in_=T.pts[:, 64 * h:64 * h + 64]).then_inc(T.sem.dP, 16)
+    for lo, q in enumerate((syn, sca)):
+        q.dma_start(out=T.pin[64 * lo:64 * lo + 48, :], in_=T.pts[:, :]).then_inc(T.sem.dP, 16)
     syn.dma_start(out=T.wt[:, :], in_=T.nodes[7::16, :]).then_inc(T.sem.dW, 16)
-    sca.dma_start(out=T.sk[:, :], in_=T.nodes[6::16, :]).then_inc(T.sem.dS, 16)
+    for e in range(2):
+        sca.dma_start(out=T.sk[:, e, :], in_=T.nodes[6 + 16 * e::32, :]).then_inc(T.sem.dS, 16)
     vwait(syn, "m0")
     vwait(sca, "m0")
-    for gg in range(8):
-        q = syn if gg < 4 else sca
-        q.dma_start(out=T.basei[16 * gg:16 * gg + 13, 1024:2047], in_=T.nodes[16 * gg:16 * gg + 13, 1025:2048]).then_inc(T.sem.dU, 16)
-    syn.dma_start(out=T.n1[:, :], in_=T.nodes[:, 0:8]).then_inc(T.sem.dN, 16)
-    syn.dma_start(out=T.n0[6:128, :], in_=T.nodes[0:122, 0:8]).then_inc(T.sem.dN, 16)
-    syn.dma_start(out=T.n0[0:6, :], in_=T.nodes[8:14, 0:8]).then_inc(T.sem.dN, 16)
-    vwait(syn, "pa", "ph", "pl")
-    for k, name in ((13, "pa"), (14, "ph"), (15, "pl")):
-        syn.dma_start(out=T.basei[k::16, 0:2048], in_=T[name][:, :]).then_inc(T.sem.dPc, 16)
     for a in range(6):
-        syn.dma_start(out=T.basei[a::16, 0:1024], in_=T.nodes[a::16, 1:1025]).then_inc(T.sem.dL, 16)
+        q = syn if a < 3 else sca
+        q.dma_start(out=T.basei[a::16, 1024:2047], in_=T.nodes[a::16, 1025:2048]).then_inc(T.sem.dU, 16)
+    for k, name in ((13, "pa"), (14, "ph"), (15, "pl")):
+        vwait(syn, name)
+        syn.dma_start(out=T.basei[k::16, 0:2048], in_=T[name][:, :]).then_inc(T.sem.dPc, 16)
+    vwait(sca, "m1")
+    for a in range(6):
+        q = syn if a < 3 else sca
+        q.dma_start(out=T.basei[a::16, 0:1024], in_=T.nodes[a::16, 1:1025]).then_inc(T.sem.dL, 16)
+    vwait(syn, "n0")
+    syn.dma_start(out=T.n0[6:128, :], in_=T.nodes[0:122, 0:8]).then_inc(T.sem.dN, 16)
 
     fl = {"allow_small_or_imprecise_dtypes": True}
     g.iota(T.coli[:, 0:1], [[0, 1]], 0, 1).then_inc(T.sem.gi0, 1)
-    g.iota(T.colp[:, 0:1], [[0, 1]], 0, -1, **fl).then_inc(T.sem.gi5, 1)
-    g.iota(T.u1[:, :], [[1, 144]], 0, 0, **fl).then_inc(T.sem.gi3, 1)
     g.iota(T.pa[:, :], [[2, 128]], 2, 256).then_inc(T.sem.gi1, 1)
+    g.iota(minus_p, [[0, 1]], -15, -1, **fl).then_inc(T.sem.gi5, 1)
+    g.iota(T.u1[:, :], [[1, 144]], 0, 0, **fl).then_inc(T.sem.gi3, 1)
     vwait(g, "pat")
-    g.iota(T.pat[:, :, 0:12], [[3, 8], [0, 4], [1, 3]], 0, 0, **fl).then_inc(T.sem.gi2, 1)
+    g.iota(T.pat[:, :, 0:12], [[6, 8], [0, 4], [2, 3]], 47, 0, **fl).then_inc(T.sem.gi2, 1)
 
     dire, shar = direct(core), shares(core)
     chip_mates = topo.cores_of(core)
     vwait(g, "msg")
     wide = topo.engines(core, shar[0][0])
     n_on = len(wide) // 2
-    rel_engs = [wide[n_on + 4 * i:n_on + 4 * i + 4] for i in range(len(shar))]
-    res_engs = [wide[8 * i:8 * i + 8] for i in range(len(shar))]
+    rel_engs = [wide[n_on + RE * i:n_on + RE * i + RE] for i in range(len(shar))]
+    res_engs = [wide[RS * i:RS * i + RS] for i in range(len(shar))]
     dir_engs, k = {}, 0
     for d in dire:
         if d in chip_mates:
@@ -342,58 +316,58 @@ def rank_program(g, core, T, topo):
                            "pa%d" % direct(d).index(core)) for d in dire], local_sem=T.sem.ls)
     g.iota(T.u2[:, :], [[1, 72], [0, 2]], 0, 0, **fl).then_inc(T.sem.gi4, 1)
     for b in ORD:
-        vwait(g, *["kr%s%d" % (b, r) for r in range(b == "A", 4)])
+        vwait(g, "kr" + b)
         if b == "B":
-            g.remote_dma_fused([tr(T.RB[:, 16 * i:16 * i + 16], T.rres[:, :], rel, res_engs[i], "rr") for i, (rel, _) in enumerate(shar)],
+            g.remote_dma_fused([tr(T.RB[:, 32 * i:32 * i + 32], T.rres[:, :], rel, res_engs[i], "rr") for i, (rel, _) in enumerate(shar)],
                                local_sem=T.sem.ls)
         else:
-            g.remote_dma_fused([tr(T.RA[:, 8 * i + 8:8 * i + 16], T.rland[:, 8 * slot(d, core) + 8:8 * slot(d, core) + 16], d, dir_engs[d], "rs")
-                                for i, d in enumerate(dire)], local_sem=T.sem.ls)
-    g.wait_ge(T.sem.ls, 12 * len(shar) + 8 * len(dire))
+            g.remote_dma_fused([tr(T.rland[:, 16 * i:16 * i + 16], home(d, core), d, dir_engs[d], "rs") for i, d in enumerate(dire)],
+                               local_sem=T.sem.ls)
+    g.wait_ge(T.sem.ls, (RE + RS) * len(shar) + 8 * len(dire))
 
     def act(out, in_, func, sem, **kw):
         sca.activation(out=out, in_=in_, func=func, **kw).then_inc(T.sem[sem], 1)
 
     def first(b):
         sca.wait_ge(T.sem["pp" + b], 8)
-        act(T["C" + b][:, :], T["pp" + b][:, :], Fn.Sign, "sy" + b, bias=cf("s01"), scale=-1.0)
-        act(T["P" + b][:, :], T["pp" + b][:, 0:NV], Fn.Copy, "pc" + b)
+        for e in range(2):
+            act(T["C" + b][:, e:512:2], T["pp" + b][:, :, e:16:2], Fn.Sign, "sy" + b, bias=cf("s01"), scale=-1.0)
+        act(T["P" + b][:, :], T["pp" + b][:, 0:NV // 16, :], Fn.Copy, "pc" + b)
 
-    sca.wait_ge(T.sem.gi3, 1)
     sca.wait_ge(T.sem.gi5, 1)
-    act(T.zt[:, 0:128], T.u1[:, 0:128], Fn.Abs, "ksb", bias=T.colp[:, 0:1])
-    sca.wait_ge(T.sem.ksb, 1)
-    act(T.idn[:, :], T.zt[:, 0:128], Fn.Relu, "ksc", bias=1.0, scale=-1.0)
-    vwait(sca, "ne", "no")
-    for k, name in ((0, "ne"), (1, "no")):
-        act(T.zt[:, 128 + 48 * k:176 + 48 * k], T.u1[:, 0:48], Fn.Abs, "ksb", bias=cf(name))
-    sca.wait_ge(T.sem.ksb, 3)
-    act(T.zs[:, :], T.zt[:, 128:224], Fn.Relu, "ksd", bias=1.0, scale=-1.0)
-    vwait(sca, "s01")
-    first("A")
+    done = 0
+    for k, (out, in_, func, bias, scale, n) in enumerate(early):
+        if k == 5:
+            sca.wait_ge(T.sem.gi2, 1)
+        if k == LP:
+            vwait(sca, "lt", "eq")
+        if n > done:
+            sca.wait_ge(T.sem.ac, n)
+            done = n
+        act(out, in_, func, "ac", bias=bias, scale=scale)
     vwait(sca, "basef")
     act(T.tab[:, 2048:4096:2], T.basef[:, :], Fn.Copy, "ht")
     act(T.tab[:, 2 * NM + 1:4096:2], T.basef[:, 0:1024].indirect(T.missl[:, NM // 16:128]), Fn.Copy, "ht", scale=below(14))
     act(T.tab[:, 0:1], T.basef[:, 1023:1024], Fn.Copy, "ht", scale=below(14))
+    vwait(sca, "s01")
+    first("A")
     first("B")
     side = [
-        (cs(NU2), cf("u"), Fn.Identity, 0.5, -0.5),
-        (cs(WZ), row(14), Fn.Identity, row(15), 256.0),
-        (T.zt[:, 224:368], T.u2[:, :], Fn.Abs, cs(NU2), 1.0),
-        (cs(NA4), cf("a"), Fn.Identity, -7.0, -4.0),
-        (T.zp[:, :], T.zt[:, 224:368], Fn.Relu, 1.0, -1.0),
-        (cs(NU3), cf("odd"), Fn.Identity, cs(NA4), 4.0),
-        (T.zw[:, :], T.zp[:, :], Fn.Copy, 0.0, cs(WZ)),
-        (T.w0r[:, :], T.u1[:, 0:64], Fn.Identity, T.colb[:, 0:1], 0.0),
-        (T.zf[:, :], T.zp[:, :], Fn.Copy, 0.0, cf("sf")),
-        (T.zt[:, 368:512], T.u2[:, :], Fn.Abs, cs(NU3), 1.0),
-        (cs(NWH), cf("wh"), Fn.Copy, 0.0, -1.0),
-        (T.zq[:, :], T.zp[:, :], Fn.Copy, 0.0, cf("xx")),
-        (T.zh[:, :], T.zt[:, 368:512], Fn.Relu, cf("wh"), cs(NWH)),
-        (cs(EV), cf("odd"), Fn.Identity, 1.0, -1.0),
+        (cs("nu2"), cf("u"), Fn.Identity, 0.5, -0.5),
+        (cs("wz"), row(14), Fn.Identity, row(15), 256.0),
+        (T.zt[:, 256:400], T.u2[:, :], Fn.Abs, cs("nu2"), 1.0),
+        (cs("na4"), cf("a"), Fn.Identity, -7.0, -4.0),
+        (T.zp[:, :], T.zt[:, 256:400], Fn.Relu, 1.0, -1.0),
+        (cs("nu3"), cf("odd"), Fn.Identity, cs("na4"), 4.0),
+        (T.zw[:, :], T.zp[:, :], Fn.Copy, 0.0, cs("wz")),
+        (T.zt[:, 400:544], T.u2[:, :], Fn.Abs, cs("nu3"), 1.0),
+        (cs("nwh"), cf("wh"), Fn.Copy, 0.0, -1.0),
+        (T.zq[:, :], T.zp[:, :], Fn.Copy, 0.0, cs("xx")),
+        (T.zh[:, :], T.zt[:, 400:544], Fn.Relu, cf("wh"), cs("nwh")),
     ]
     sca.wait_ge(T.sem.ht, 3)
     sca.wait_ge(T.sem.gi4, 1)
+    sca.wait_ge(T.sem.ac, len(early))
     k = 0
     for t in range(2, V):
         for b in ORD:
@@ -406,26 +380,12 @@ def rank_program(g, core, T, topo):
                 act(out, in_, func, "sl", bias=bias, scale=scale)
                 k += 1
 
-    vwait(ten, "skh")
-    ten.wait_ge(T.sem.ksc, 1)
-    ten.matmul(T.ppB[:, 0:128], T.skh[:, :], T.idn[:, :], True, True).then_inc(T.sem.lt, 1)
-    vwait(ten, "skt")
-    ten.wait_ge(T.sem.ksd, 1)
-    for c in range(8):
-        a = 32 * (c // 2)
-        if c % 2 == 0 and c > 0:
-            ten.wait_ge(T.sem.ll, 8 * c)
-        for gg in range(8):
-            h, z = 32 * (gg // 2), 48 * (c % 2) + 16 - 16 * (gg % 2)
-            ten.matmul(T.ppB[h:h + 32, 128 + c:256:8], T.zs[a:a + 32, z:z + 32], T.skt[a:a + 32, 16 * gg:16 * gg + 16],
-                       gg % 2 == 0, gg % 2 == 1).then_inc(T.sem.ll, 1)
-
     def spread(b, srcs):
-        for r, (buf, c0, sem) in enumerate(srcs):
+        for r, buf, c0, sem in srcs:
             if sem:
                 ten.wait_ge(T.sem[sem], 4)
             for h in range(2):
-                ten.matmul(T["pp" + b][:, 256 * h + r:256 * h + 253 + r:4], T.lp[:, 128 * h:128 * h + 128],
+                ten.matmul(T["pp" + b][:, 16 * h + r:16 * h + 16:4, :], T.lp[:, 128 * h:128 * h + 128],
                            T[buf][:, c0:c0 + 64], True, True).then_inc(T.sem["pp" + b], 1)
 
     def tx(b, t, js):
@@ -444,15 +404,15 @@ def rank_program(g, core, T, topo):
         return lambda p: dcol(b, t, 64 * p, 64 * p + 64)
 
     nd, nx = len(dire), len(cross(core))
-    vwait(ten, "lp0", "lp1", "msg")
-    spread("A", [("msg", 0, None)] + [("land", 64 * i, "pa%d" % i) for i in range(nd)])
+    ten.wait_ge(T.sem.ac, LP)
+    vwait(ten, "msg")
+    spread("A", [(nd, "msg", 0, None)] + [(i, "land", 64 * i, "pa%d" % i) for i in range(nd)])
+    spread("B", [(i, "land", 64 * (nd + i), "pb%d" % i) for i in range(nx)])
     vwait(ten, "zx")
-    ten.wait_ge(T.sem.syA, 1)
-    tx("A", 1, range(16))
-    vwait(ten, "missl")
-    spread("B", [("land", 64 * (nd + i), "pb%d" % i) for i in range(nx)])
-    ten.wait_ge(T.sem.syB, 1)
-    tx("B", 1, range(16))
+    for b in "AB":
+        for e in range(2):
+            ten.wait_ge(T.sem["sy" + b], e + 1)
+            tx(b, 1, range(e, 16, 2))
     for t in range(2, V):
         for b in ORD:
             W = T["W" + b][:, 0:64]
@@ -461,18 +421,12 @@ def rank_program(g, core, T, topo):
                     vwait(ten, "sub%d%s%d" % (e, b, t))
                     tx(b, t, range(e, 16, 2))
             if t == 6 and b == B1:
-                ten.wait_ge(T.sem.sl, 8)
-                pairs(T.psm[:, 0:1], "zw", lambda p: T.colb[:, 1:2], "w47", True, True)
-            if t == 7:
-                pairs(W, "zw", lambda p: T.w0r[:, :], "wb" + b, True, False)
-            if t == 8:
-                ten.wait_ge(T.sem.sl, 9)
-                o = 8 if b == "A" else 72
-                pairs(T.psm[:, o:o + 64], "zf", blocks("C" + b), "qo" + b, True, True)
+                ten.wait_ge(T.sem.sl, 7)
+                pairs(T.psm[:, 0:1], "zw", lambda p: T.colb[:, 0:1], "w47", True, True)
             if t == 11:
-                ten.wait_ge(T.sem.sl, 13)
+                ten.wait_ge(T.sem.sl, len(side))
                 ten.wait_ge(T.sem["hx" + b], 128)
-                pairs(W, "zh", blocks("h1" + b), "wb" + b, False, False)
+                pairs(W, "zh", blocks("h1" + b), "wb" + b, True, False)
             if t == 12:
                 pairs(W, "zw", visit(b, t), "wb" + b, False, False)
             if t == 13:
@@ -492,5 +446,5 @@ def rank_program(g, core, T, topo):
                 syn.dma_start(out=T[dst + b][k + 16 * e:k + 16 * e + 16, :],
                               in_=T["D" + b][14 + e::16, 512 * (t - 2):512 * t]).then_inc(T.sem[sem + b], 16)
     vwait(syn, "ys")
-    syn.dma_start(out=T.y[:, :], in_=T.ysum[:, :]).then_inc(T.sem.dY, 16)
+    syn.dma_start(out=T.y[:, :], in_=T.ysum[0:128:2, :]).then_inc(T.sem.dY, 16)
     syn.wait_ge(T.sem.dY, 16)

from concourse.bass import DstId, RemoteDMATransfer
from concourse.mybir import AluOpType as Op, ActivationFunctionType as Fn

V = 15
ORD = "AB"
B0, B1 = ORD
NV = 352
NM = 1472
RE, RS = 4, 8
U = 2.0 ** -46
KV = 11.0 * 2 ** 18
SCRATCH = {
    "pin": ("sbuf", [128, 64], "int32"), "pq": ("sbuf", [128, 64], "int32"), "msg": ("sbuf", [128, 64], "float16"),
    "land": ("sbuf", [128, 448], "float16"), "rmsg": ("sbuf", [128, 64], "float16"), "rres": ("sbuf", [128, 32], "float32"),
    "coli": ("sbuf", [128, 16], "int32"), "colf": ("sbuf", [128, 64], "float32"), "colb": ("sbuf", [128, 8], "bfloat16"),
    "colp": ("sbuf", [128, 8], "float32"), "cols": ("sbuf", [128, 32], "float32"),
    "pat": ("sbuf", [128, 8, 16], "float32"), "lt": ("sbuf", [128, 16], "float32"), "eq": ("sbuf", [128, 16], "float32"),
    "u1": ("sbuf", [128, 144], "float32"), "u2": ("sbuf", [128, 144], "float32"),
    "lp": ("sbuf", [128, 256], "bfloat16"), "zt": ("sbuf", [128, 544], "float32"),
    "zx": ("sbuf", [128, 144], "bfloat16"), "zw": ("sbuf", [128, 144], "bfloat16"),
    "zq": ("sbuf", [128, 144], "bfloat16"), "zh": ("sbuf", [128, 144], "bfloat16"), "zp": ("sbuf", [128, 144], "bfloat16"),
    "sk": ("sbuf", [128, 2, 64], "int32"), "skf": ("sbuf", [128, 2, 64], "float32"), "skw": ("sbuf", [128, 128], "float32"),
    "wt": ("sbuf", [128, 128], "int32"), "n0": ("sbuf", [128, 8], "int32"),
    "pa": ("sbuf", [128, 128], "int32"), "ph": ("sbuf", [128, 128], "int32"), "pl": ("sbuf", [128, 128], "int32"),
    "missl": ("sbuf", [128, 128], "uint16"),
    "basei": ("sbuf", [128, 2048], "int32"), "basef": ("sbuf", [128, 1024], "float32"),
    "tab": ("sbuf", [128, 4096], "float32"),
    "rland": ("sbuf", [128, 176], "float32"), "RB": ("sbuf", [128, 64], "float32"),
    "s64": ("sbuf", [128, 64], "float32"), "s32": ("sbuf", [128, 32], "float32"), "ysum": ("sbuf", [128, 16], "float32"),
    "psm": ("psum", [128, 8], "float32"),
}
SEMAPHORES = ["vc", "ac", "gi0", "gi1", "gi2", "gi3", "gi4", "gi5", "dP", "dS", "dW", "dN", "dU", "dL", "dPc", "dY",
              "ht", "w47", "sl", "pa0", "pa1", "pa2", "pb0", "pb1", "pb2", "pb3", "rs", "rm", "rr", "ls", "rl"]
for _b in "AB":
    SCRATCH.update({
        "off" + _b: ("sbuf", [128, 32], "uint16"), "P" + _b: ("sbuf", [128, NV], "float32"), "G" + _b: ("sbuf", [128, 512 - NV], "float32"),
        "D" + _b: ("sbuf", [128, 512 * (V - 2)], "float16"), "C" + _b: ("sbuf", [128, 512], "bfloat16"),
        "h1" + _b: ("sbuf", [128, 512], "float16"), "h2" + _b: ("sbuf", [128, 512], "float16"),
        "t1" + _b: ("sbuf", [128, 64], "float32"),
        "pp" + _b: ("psum", [128, 32, 16], "float32"), "X" + _b: ("psum", [128, 64], "float32"), "W" + _b: ("psum", [128, 64], "float32"),
    })
    SEMAPHORES += [k + _b for k in ("pp", "pc", "sy", "s", "x", "wb", "q", "hx", "hz")]


def mask_of(engs):
    m = 0
    for e in engs:
        m |= 1 << e
    return m


def rank_program(g, core, T, topo):
    cores = list(T.cores)

    def direct(c):
        return [d for d in cores if d != c and topo.may_write(c, d)]

    def cross(c):
        return [d for d in cores if d != c and not topo.may_write(c, d)]

    def shares(c):
        x = cross(c)
        rl = [k for k in topo.cores_of(c) if k not in cores and topo.die(k) == topo.die(c) and all(topo.may_write(k, d) for d in x)][:2]
        n = -(-len(x) // len(rl))
        return [(k, x[i * n:(i + 1) * n]) for i, k in enumerate(rl)]

    def slot(dst, src):
        return (direct(dst) + cross(dst)).index(src)

    def home(dst, src):
        return T.rland[:, 16 * slot(dst, src) + 64:16 * slot(dst, src) + 80]

    def tr(src_ap, dst_ap, dst, engs, sem):
        rid, pid = topo.addr(dst, core)
        return RemoteDMATransfer(dst_ids=[DstId(rid=rid, pnc=pid)], dma_engine_mask=mask_of(engs), remote_sem=T.sem[sem],
                                 srcs=[src_ap], dsts=[dst_ap], alu_op=0)

    if T.rank_of(core) is None:
        for c in cores:
            for k, (rel, dests) in enumerate(shares(c)):
                if rel != core:
                    continue
                engs = [topo.engines(core, d)[4 * i:4 * i + 4] for i, d in enumerate(dests)]
                g.wait_ge(T.sem.rm, RE)
                g.remote_dma_fused([tr(T.rmsg[:, :], T.land[:, 64 * slot(d, c):64 * slot(d, c) + 64], d, engs[i],
                                       "pb%d" % cross(d).index(c)) for i, d in enumerate(dests)], local_sem=T.sem.rl)
                g.wait_ge(T.sem.rr, RS)
                g.remote_dma_fused([tr(T.rres[:, 16 * i:16 * i + 16], home(d, c), d, engs[i], "rs") for i, d in enumerate(dests)],
                                   local_sem=T.sem.rl)
                g.wait_ge(T.sem.rl, 16)
        return

    vec, ten, sca, syn = g.vector, g.tensor, g.scalar, g.sync
    nv, seen, made = [0], [0], {}

    def v(name, ins):
        ins.then_inc(T.sem.vc, 1)
        nv[0] += 1
        made[name] = nv[0]

    def need(*names):
        n = max(made[k] for k in names)
        if n > seen[0]:
            vec.wait_ge(T.sem.vc, n)
            seen[0] = n

    def vwait(q, *names):
        q.wait_ge(T.sem.vc, max(made[k] for k in names))

    def ts(out, in0, s1, op0, s2=None, op1=None):
        if op1 is None:
            return vec.tensor_scalar(out=out, in0=in0, scalar1=s1, scalar2=None, op0=op0)
        return vec.tensor_scalar(out=out, in0=in0, scalar1=s1, scalar2=s2, op0=op0, op1=op1)

    def tt(out, a, b, op):
        return vec.tensor_tensor(out=out, in0=a, in1=b, op=op)

    col, scol = {}, {}

    def cf(name):
        k = col.setdefault(name, len(col) + 1)
        return T.colf[:, k:k + 1]

    def cs(name):
        k = scol.setdefault(name, len(scol))
        return T.cols[:, k:k + 1]

    def ci(k):
        return T.coli[:, k:k + 1]

    def below(k):
        return T.lt[:, k:k + 1]

    def row(k):
        return T.eq[:, k:k + 1]

    def dcol(b, t, a=0, z=512, s=1):
        return T["D" + b][:, 512 * (t - 2) + a:512 * (t - 2) + z:s]

    minus_p = T.colp[:, 0:1]
    early = [
        (cs("hi"), minus_p, Fn.Sign, -78.5, -1.0, 0),
        (cs("w"), cs("hi"), Fn.Identity, 512.5 * U, -511.5 * U, 1),
        (cs("k0"), cs("hi"), Fn.Identity, minus_p, 32.0, 1),
        (cs("nw"), cs("hi"), Fn.Identity, -512.5 * U, 511.5 * U, 1),
        (cs("k1"), cs("k0"), Fn.Identity, 1.0, 1.0, 3),
        (T.zt[:, 0:128], T.pat[:, :, :], Fn.Abs, cs("k0"), 1.0, 3),
        (T.zt[:, 128:256], T.pat[:, :, :], Fn.Abs, cs("k1"), 1.0, 5),
        (T.lp[:, :], T.zt[:, 0:256], Fn.Relu, cs("w"), cs("nw"), 7),
        (cs("n6"), below(6), Fn.Copy, 0.0, -1.0, 7),
        (cs("c0"), below(12), Fn.Copy, 0.0, U, 7),
        (cs("sg"), below(3), Fn.Identity, cs("n6"), 2.0, 9),
        (cs("sa"), below(9), Fn.Identity, cs("n6"), 2.0, 9),
        (cs("xa"), cs("sg"), Fn.Identity, row(13), KV, 11),
        (cs("sh"), cs("sg"), Fn.Copy, 0.0, -U / 2, 11),
        (cs("sf"), below(12), Fn.Identity, cs("sa"), -1.0, 12),
        (cs("wr"), row(14), Fn.Identity, row(15), 1.0, 12),
        (cs("sb"), cs("sf"), Fn.Identity, cs("sh"), -U / 2, 15),
        (cs("xx"), cs("sf"), Fn.Identity, cs("xa"), -32 * KV, 15),
    ]
    COLS, LP = len(early), 8

    def cv(name, in0, *args, deps=()):
        if deps:
            need(*deps)
        v(name, ts(cf(name), in0, *args))

    def iv(k, *args):
        v("i%d" % k, ts(ci(k), ci(0), *args))

    v("m0", vec.memset(T.basei[:, 1024:2048], 0))
    v("pat", vec.memset(T.pat[:, :, :], -99.0))
    v("pq", vec.memset(T.pq[:, :], 0))
    v("m1", vec.memset(T.basei[:, 0:1024], 0))
    vec.wait_ge(T.sem.gi1, 1)
    v("pa", ts(T.pa[:, :], T.pa[:, :], 4095, Op.bitwise_and))
    vec.wait_ge(T.sem.dP, 32)
    need("pq")
    v("q0", ts(T.pq[0:48, :], T.pin[0:48, :], 10, Op.arith_shift_right))
    v("q1", ts(T.pq[64:112, :], T.pin[64:112, :], 1023, Op.bitwise_and))
    vec.wait_ge(T.sem.gi0, 1)
    iv(1, 15, Op.bitwise_and)
    need("q0", "q1")
    v("msg", vec.tensor_copy(out=T.msg[:, :], in_=T.pq[:, :]))
    vec.wait_ge(T.sem.dW, 16)
    v("ph", ts(T.ph[:, :], T.wt[:, :], 8, Op.arith_shift_right))
    v("pl", ts(T.pl[:, :], T.wt[:, :], 255, Op.bitwise_and))
    cv("a", ci(1), 1.0, Op.mult, deps=["i1"])
    v("n0", vec.memset(T.n0[:, :], 0))
    vec.wait_ge(T.sem.gi3, 1)
    need("a")
    v("lt", ts(T.lt[:, :], T.u1[:, 0:16], cf("a"), Op.is_gt))
    v("eq", ts(T.eq[:, :], T.u1[:, 0:16], cf("a"), Op.is_equal))
    vec.wait_ge(T.sem.dS, 32)
    v("skf", ts(T.skf[:, :, :], T.sk[:, :, :], -1.0, Op.add))
    cv("sm", below(6), U, Op.mult, row(13), Op.add, deps=["eq"])
    cv("g0", below(6), 2.0 ** -25 + U / 2, Op.mult)
    need("skf")
    for b in range(4):
        v("skw", vec.transpose(out=T.skw[:, b:128:4], in_=T.skf[:, :, 16 * b:16 * b + 16]))
    cv("sc", cf("sm"), row(14), Op.add, row(15), Op.add, deps=["g0"])
    cv("ng", below(3), -U, Op.mult, cf("g0"), Op.add)
    need("skw")
    v("ml0", vec.tensor_copy(out=T.missl[:, 0:64], in_=T.skw[:, 0:64]))
    v("missl", ts(T.missl[:, 64:128], T.skw[:, 64:128], -1024.0, Op.add))
    cv("u", ci(0), cf("a"), Op.subtract, 15.0, Op.add)

    vec.wait_ge(T.sem.dU, 96)
    vec.wait_ge(T.sem.dPc, 48)
    need("missl")
    v("basef", ts(T.basef[:, :], T.basei[:, 1024:2048], cf("sc"), Op.mult, cf("ng"), Op.add))
    v("missU", ts(T.tab[:, 2049:2 * NM:2], T.basei[:, 1024:2048].indirect(T.missl[:, 64:NM // 16]), cf("sm"), Op.mult, cf("ng"), Op.add))
    vec.wait_ge(T.sem.ac, COLS)
    need("u")
    v("zx", ts(T.zx[:, :], T.u1[:, 0:144], cf("u"), Op.is_equal, cs("xx"), Op.mult))
    vec.wait_ge(T.sem.dL, 96)
    cv("s1", T.basei[:, 0:1], cf("sm"), Op.mult, cs("sb"), Op.add)
    vec.wait_ge(T.sem.dN, 16)
    cv("s01", T.n0[:, 0:1], cs("c0"), Op.mult, cf("s1"), Op.add, deps=["s1"])
    cv("w0", T.basei[:, 0:1], cs("wr"), Op.mult)
    v("hitL", ts(T.tab[:, 2:2048:2], T.basei[:, 1:1024], cf("sc"), Op.mult, cf("ng"), Op.add))
    v("tab", ts(T.tab[:, 1:2048:2], T.basei[:, 0:2048].indirect(T.missl[:, 0:64]), cf("sm"), Op.mult, cf("ng"), Op.add))
    iv(4, 1, Op.bitwise_and)
    iv(8, 4, Op.arith_shift_right, 1, Op.bitwise_and)
    v("colb", vec.tensor_copy(out=T.colb[:, 0:1], in_=T.basei[:, 2047:2048]))
    cv("odd", ci(4), 1.0, Op.mult, deps=["i4"])
    v("tab", ts(T.tab[:, 2:4], T.tab[:, 2:4], cf("w0"), Op.add))
    cv("wh", ci(8), -255.0, Op.mult, 256.0, Op.add, deps=["i8"])

    def sub(b, t, e):
        v("sub%d%s%d" % (e, b, t), tt(dcol(b, t, NV + e, 512, 2), T["G" + b][:, e:512 - NV:2], T["pp" + b][:, NV // 16:32, e:16:2], Op.subtract))

    vec.wait_ge(T.sem.ht, 3)
    need("tab")
    last = None
    for t in range(2, V):
        for b in ORD:
            if t == 2:
                vec.wait_ge(T.sem["pc" + b], 1)
            vec.wait_ge(T.sem["x" + b], 16 * (t - 1))
            off = "off%s%d" % (b, t)
            if t == 2:
                v(off, ts(T["off" + b][:, :], T["X" + b][:, 0:32], 2.0 ** -25, Op.mult, 2.921875 - 16.5, Op.add))
            else:
                v(off, ts(T["off" + b][:, :], T["X" + b][:, 0:32], 0.921875, Op.add))
            if last:
                sub(*last, 1)
            need(off)
            v("gv", tt(dcol(b, t, 0, NV), T.tab[:, 0:4096].indirect(T["off" + b][:, 0:NV // 16]), T["P" + b][:, :], Op.subtract))
            vec.wait_ge(T.sem["s" + b], t - 1)
            sub(b, t, 0)
            last = (b, t)
    sub(*last, 1)
    vec.wait_ge(T.sem.w47, 8)
    v("w47", vec.tensor_copy(out=T.colf[:, 0:1], in_=T.psm[:, 0:1]))

    for b in ORD:
        vec.wait_ge(T.sem["q" + b], 8)
        need("w47")
        v("t1", ts(T["t1" + b][:, :], T["X" + b][:, 0:64], 4093.484375, Op.is_equal, T.colf[:, 0:1], Op.mult))
        vec.wait_ge(T.sem["wb" + b], 40)
        need("t1")
        v("kr" + b, tt(T.rland[:, 0:64] if b == "A" else T.RB[:, :], T["W" + b][:, 0:64], T["t1" + b][:, :], Op.add))
    need("krA")
    vec.wait_ge(T.sem.rs, 4 * 7)
    v("s64", tt(T.s64[:, :], T.rland[:, 48:112], T.rland[:, 112:176], Op.add))
    need("s64")
    v("s32", tt(T.s32[:, :], T.s64[:, 0:32], T.s64[:, 32:64], Op.add))
    need("s32")
    v("ys", tt(T.ysum[:, :], T.s32[:, 0:16], T.s32[:, 16:32], Op.add))

    for lo, q in enumerate((syn, sca)):
        q.dma_start(out=T.pin[64 * lo:64 * lo + 48, :], in_=T.pts[:, :]).then_inc(T.sem.dP, 16)
    syn.dma_start(out=T.wt[:, :], in_=T.nodes[7::16, :]).then_inc(T.sem.dW, 16)
    for e in range(2):
        sca.dma_start(out=T.sk[:, e, :], in_=T.nodes[6 + 16 * e::32, :]).then_inc(T.sem.dS, 16)
    vwait(syn, "m0")
    vwait(sca, "m0")
    for a in range(6):
        q = syn if a < 3 else sca
        q.dma_start(out=T.basei[a::16, 1024:2047], in_=T.nodes[a::16, 1025:2048]).then_inc(T.sem.dU, 16)
    for k, name in ((13, "pa"), (14, "ph"), (15, "pl")):
        vwait(syn, name)
        syn.dma_start(out=T.basei[k::16, 0:2048], in_=T[name][:, :]).then_inc(T.sem.dPc, 16)
    vwait(sca, "m1")
    for a in range(6):
        q = syn if a < 3 else sca
        q.dma_start(out=T.basei[a::16, 0:1024], in_=T.nodes[a::16, 1:1025]).then_inc(T.sem.dL, 16)
    vwait(syn, "n0")
    syn.dma_start(out=T.n0[6:128, :], in_=T.nodes[0:122, 0:8]).then_inc(T.sem.dN, 16)

    fl = {"allow_small_or_imprecise_dtypes": True}
    g.iota(T.coli[:, 0:1], [[0, 1]], 0, 1).then_inc(T.sem.gi0, 1)
    g.iota(T.pa[:, :], [[2, 128]], 2, 256).then_inc(T.sem.gi1, 1)
    g.iota(minus_p, [[0, 1]], -15, -1, **fl).then_inc(T.sem.gi5, 1)
    g.iota(T.u1[:, :], [[1, 144]], 0, 0, **fl).then_inc(T.sem.gi3, 1)
    vwait(g, "pat")
    g.iota(T.pat[:, :, 0:12], [[6, 8], [0, 4], [2, 3]], 47, 0, **fl).then_inc(T.sem.gi2, 1)

    dire, shar = direct(core), shares(core)
    chip_mates = topo.cores_of(core)
    vwait(g, "msg")
    wide = topo.engines(core, shar[0][0])
    n_on = len(wide) // 2
    rel_engs = [wide[n_on + RE * i:n_on + RE * i + RE] for i in range(len(shar))]
    res_engs = [wide[RS * i:RS * i + RS] for i in range(len(shar))]
    dir_engs, k = {}, 0
    for d in dire:
        if d in chip_mates:
            dir_engs[d] = wide[n_on:n_on + 4]
        else:
            dir_engs[d] = topo.engines(core, d)[4 * k:4 * k + 4]
            k += 1
    g.remote_dma_fused([tr(T.msg[:, :], T.rmsg[:, :], rel, rel_engs[i], "rm") for i, (rel, _) in enumerate(shar)], local_sem=T.sem.ls)
    g.remote_dma_fused([tr(T.msg[:, :], T.land[:, 64 * slot(d, core):64 * slot(d, core) + 64], d, dir_engs[d],
                           "pa%d" % direct(d).index(core)) for d in dire], local_sem=T.sem.ls)
    g.iota(T.u2[:, :], [[1, 72], [0, 2]], 0, 0, **fl).then_inc(T.sem.gi4, 1)
    for b in ORD:
        vwait(g, "kr" + b)
        if b == "B":
            g.remote_dma_fused([tr(T.RB[:, 32 * i:32 * i + 32], T.rres[:, :], rel, res_engs[i], "rr") for i, (rel, _) in enumerate(shar)],
                               local_sem=T.sem.ls)
        else:
            g.remote_dma_fused([tr(T.rland[:, 16 * i:16 * i + 16], home(d, core), d, dir_engs[d], "rs") for i, d in enumerate(dire)],
                               local_sem=T.sem.ls)
    g.wait_ge(T.sem.ls, (RE + RS) * len(shar) + 8 * len(dire))

    def act(out, in_, func, sem, **kw):
        sca.activation(out=out, in_=in_, func=func, **kw).then_inc(T.sem[sem], 1)

    def first(b):
        sca.wait_ge(T.sem["pp" + b], 8)
        for e in range(2):
            act(T["C" + b][:, e:512:2], T["pp" + b][:, :, e:16:2], Fn.Sign, "sy" + b, bias=cf("s01"), scale=-1.0)
        act(T["P" + b][:, :], T["pp" + b][:, 0:NV // 16, :], Fn.Copy, "pc" + b)

    sca.wait_ge(T.sem.gi5, 1)
    done = 0
    for k, (out, in_, func, bias, scale, n) in enumerate(early):
        if k == 5:
            sca.wait_ge(T.sem.gi2, 1)
        if k == LP:
            vwait(sca, "lt", "eq")
        if n > done:
            sca.wait_ge(T.sem.ac, n)
            done = n
        act(out, in_, func, "ac", bias=bias, scale=scale)
    vwait(sca, "basef")
    act(T.tab[:, 2048:4096:2], T.basef[:, :], Fn.Copy, "ht")
    act(T.tab[:, 2 * NM + 1:4096:2], T.basef[:, 0:1024].indirect(T.missl[:, NM // 16:128]), Fn.Copy, "ht", scale=below(14))
    act(T.tab[:, 0:1], T.basef[:, 1023:1024], Fn.Copy, "ht", scale=below(14))
    vwait(sca, "s01")
    first("A")
    first("B")
    side = [
        (cs("nu2"), cf("u"), Fn.Identity, 0.5, -0.5),
        (cs("wz"), row(14), Fn.Identity, row(15), 256.0),
        (T.zt[:, 256:400], T.u2[:, :], Fn.Abs, cs("nu2"), 1.0),
        (cs("na4"), cf("a"), Fn.Identity, -7.0, -4.0),
        (T.zp[:, :], T.zt[:, 256:400], Fn.Relu, 1.0, -1.0),
        (cs("nu3"), cf("odd"), Fn.Identity, cs("na4"), 4.0),
        (T.zw[:, :], T.zp[:, :], Fn.Copy, 0.0, cs("wz")),
        (T.zt[:, 400:544], T.u2[:, :], Fn.Abs, cs("nu3"), 1.0),
        (cs("nwh"), cf("wh"), Fn.Copy, 0.0, -1.0),
        (T.zq[:, :], T.zp[:, :], Fn.Copy, 0.0, cs("xx")),
        (T.zh[:, :], T.zt[:, 400:544], Fn.Relu, cf("wh"), cs("nwh")),
    ]
    sca.wait_ge(T.sem.ht, 3)
    sca.wait_ge(T.sem.gi4, 1)
    sca.wait_ge(T.sem.ac, len(early))
    k = 0
    for t in range(2, V):
        for b in ORD:
            vwait(sca, "off%s%d" % (b, t))
            act(T["G" + b][:, :], T.tab[:, 0:4096].indirect(T["off" + b][:, NV // 16:32]), Fn.Copy, "s" + b)
            if k < len(side):
                if k > 0:
                    sca.wait_ge(T.sem.sl, k)
                out, in_, func, bias, scale = side[k]
                act(out, in_, func, "sl", bias=bias, scale=scale)
                k += 1

    def spread(b, srcs):
        for r, buf, c0, sem in srcs:
            if sem:
                ten.wait_ge(T.sem[sem], 4)
            for h in range(2):
                ten.matmul(T["pp" + b][:, 16 * h + r:16 * h + 16:4, :], T.lp[:, 128 * h:128 * h + 128],
                           T[buf][:, c0:c0 + 64], True, True).then_inc(T.sem["pp" + b], 1)

    def tx(b, t, js):
        for j in js:
            src = T["C" + b][:, j:512:16] if t == 1 else dcol(b, t, j, 512, 16)
            ten.matmul(T["X" + b][:, 0:32], T.zx[:, 15 - j:143 - j], src, j == 0, j == 15).then_inc(T.sem["x" + b], 1)

    def pairs(out, z, src, sem, start, stop, k=128):
        for p in range(8):
            ten.matmul(out, T[z][0:k, 14 - 2 * p:142 - 2 * p], src(p), start and p == 0, stop and p == 7).then_inc(T.sem[sem], 1)

    def blocks(name, k=128):
        return lambda p: T[name][0:k, 64 * p:64 * p + 64]

    def visit(b, t):
        return lambda p: dcol(b, t, 64 * p, 64 * p + 64)

    nd, nx = len(dire), len(cross(core))
    ten.wait_ge(T.sem.ac, LP)
    vwait(ten, "msg")
    spread("A", [(nd, "msg", 0, None)] + [(i, "land", 64 * i, "pa%d" % i) for i in range(nd)])
    spread("B", [(i, "land", 64 * (nd + i), "pb%d" % i) for i in range(nx)])
    vwait(ten, "zx")
    for b in "AB":
        for e in range(2):
            ten.wait_ge(T.sem["sy" + b], e + 1)
            tx(b, 1, range(e, 16, 2))
    for t in range(2, V):
        for b in ORD:
            W = T["W" + b][:, 0:64]
            if t < V - 1:
                for e in range(2):
                    vwait(ten, "sub%d%s%d" % (e, b, t))
                    tx(b, t, range(e, 16, 2))
            if t == 6 and b == B1:
                ten.wait_ge(T.sem.sl, 7)
                pairs(T.psm[:, 0:1], "zw", lambda p: T.colb[:, 0:1], "w47", True, True)
            if t == 11:
                ten.wait_ge(T.sem.sl, len(side))
                ten.wait_ge(T.sem["hx" + b], 128)
                pairs(W, "zh", blocks("h1" + b), "wb" + b, True, False)
            if t == 12:
                pairs(W, "zw", visit(b, t), "wb" + b, False, False)
            if t == 13:
                ten.wait_ge(T.sem["hz" + b], 32)
                pairs(W, "zh", blocks("h2" + b, 32), "wb" + b, False, False, 32)
            if t == V - 1:
                pairs(W, "zw", visit(b, t - 1), "wb" + b, False, False)
                vwait(ten, "sub1%s%d" % (b, t))
                pairs(T["X" + b][:, 0:64], "zq", visit(b, t), "q" + b, True, True)
                pairs(W, "zw", visit(b, t), "wb" + b, False, True)

    for t in range(2, 12, 2):
        for b in ORD:
            vwait(syn, "sub1%s%d" % (b, t + 1))
            dst, k, sem = ("h1", 16 * (t - 2), "hx") if t < 10 else ("h2", 0, "hz")
            for e in range(2):
                syn.dma_start(out=T[dst + b][k + 16 * e:k + 16 * e + 16, :],
                              in_=T["D" + b][14 + e::16, 512 * (t - 2):512 * t]).then_inc(T.sem[sem + b], 16)
    vwait(syn, "ys")
    syn.dma_start(out=T.y[:, :], in_=T.ysum[0:128:2, :]).then_inc(T.sem.dY, 16)
    syn.wait_ge(T.sem.dY, 16)
